import numpy as np
import ml_dtypes


def mxq(x, axis, fmt="e4m3"):
    dtype, down = {"e4m3": (ml_dtypes.float8_e4m3fn, 7), "e5m2": (ml_dtypes.float8_e5m2, 14)}[fmt]
    v = np.moveaxis(np.asarray(x, np.float32).astype(ml_dtypes.bfloat16).astype(np.float64), axis, -1)
    blocks = v.reshape(v.shape[:-1] + (-1, 32))
    amax = np.abs(blocks).max(-1, keepdims=True)
    byte = np.maximum(np.where(amax > 0, np.frexp(amax)[1] - 1 + 127, 0) - down, 1)
    scale = np.exp2(byte - 127.0)
    codes = (blocks / scale).astype(np.float32).astype(dtype).astype(np.float64)
    return np.moveaxis((codes * scale).reshape(v.shape), -1, axis)


WIDE = False


def mx_kscale(k):
    if not WIDE:
        return np.ones(k)
    levels = np.array([10, -10, 5, -5, 0])
    if k % 512:
        return np.exp2(np.random.permutation(np.resize(levels, k // 32))).repeat(32)
    a = np.empty((k // 512, 16))
    for p in range(k // 512):
        a[p, :8] = np.random.permutation(np.resize(levels, 8))
        for g in range(8):
            far = levels[np.abs(levels - a[p, g]) >= 10]
            a[p, g + 8] = far[np.random.randint(len(far))]
    return np.exp2(a.ravel()).repeat(32)


def f64(x):
    return np.asarray(x).astype(np.float64)


def striped(idx):
    return np.tile(idx.reshape(-1, 16).T, (8, 1)).astype(np.uint16)


def unstriped(offs):
    return offs[:16].T.reshape(-1).astype(np.int64)


def pack_weight(w):
    k, n = w.shape
    w = f64(np.asarray(w, np.float32).astype(ml_dtypes.bfloat16)).reshape(k // 32, 32, n)
    amax = np.abs(w).max(1)
    byte = np.clip(np.where(amax > 0, np.frexp(amax)[1] - 1 + 127 - 7, 1), 1, 254)
    scaled = (w * np.exp2(127.0 - byte)[:, None, :]).reshape(k, n).astype(np.float32)
    words = np.ascontiguousarray(scaled.reshape(k // 512, 128, 4, n).transpose(0, 1, 3, 2)).astype(ml_dtypes.float8_e4m3fn).view(np.uint8)
    return words, np.ascontiguousarray(byte.astype(np.uint8).reshape(k // 512, 16, n))


def unpack_weight(words, scales):
    g, p, n, _ = words.shape
    vals = np.ascontiguousarray(words).view(ml_dtypes.float8_e4m3fn).astype(np.float64) * np.repeat(np.exp2(scales.astype(np.float64) - 127.0), 8, axis=1)[..., None]
    return vals.transpose(0, 1, 3, 2).reshape(g * 512, n)


K, T, S, V = 512, 2048, 512, 512
P = 2 ** 7


def setup_inputs():
    n = np.random.standard_normal
    s = mx_kscale(K)[:, None]
    packed_xT = pack_weight(n((K, T)) * s)
    return {
        "x_words": packed_xT[0],
        "x_scales": packed_xT[1],
        "w1": (n((K, K)) / K / s / s.T).astype(np.float32),
        "ment": (np.tile(0.5 * np.random.standard_normal(T), (P, 1))).astype(np.float32),
        "offs": striped(np.random.permutation(T)[:S]),
        "ant": striped(np.random.permutation(T)[:V]),
    }


def reference(x_words, x_scales, w1, ment, offs, ant):
    xq = unpack_weight(x_words, x_scales)[:, unstriped(offs)]
    z = mxq(f64(w1), 0, "e4m3").T @ xq
    x_ant = unpack_weight(x_words, x_scales)[:, unstriped(ant)]
    y = (mxq(z, 0, "e4m3").T @ x_ant) + f64(ment)[:1][:, unstriped(ant)]
    e = np.exp(y - y.max(axis=1, keepdims=True))
    return e / e.sum(axis=1, keepdims=True)

@@ -1,0 +1,155 @@
+from contextlib import ExitStack
+
+import concourse.mybir as mybir
+
+K, T, S, V = 512, 2048, 512, 512
+FLOPS = 2 * K * K * S + 2 * K * S * V
+
+F32 = mybir.dt.float32
+BF16 = mybir.dt.bfloat16
+I32 = mybir.dt.int32
+U32 = mybir.dt.uint32
+U16 = mybir.dt.uint16
+U8 = mybir.dt.uint8
+FP8X4 = mybir.dt.float8_e4m3fn_x4
+ALU = mybir.AluOpType
+ACT = mybir.ActivationFunctionType
+
+P = 128
+PACK = 4
+GROUP = 16
+TILES = S // P
+
+
+def tile_picked_zcoref_soft_p_kernel(tc, x_words, x_scales, w1, ment, offs, ant, out):
+    nc = tc.nc
+    with ExitStack() as ctx:
+        keep = ctx.enter_context(tc.tile_pool(name="keep", bufs=1))
+        psum = ctx.enter_context(tc.psum_pool(name="psum", bufs=8))
+
+        offs_t = keep.tile([P, S // GROUP], U16, name="offs_t")
+        ant_t = keep.tile([P, V // GROUP], U16, name="ant_t")
+        nc.sync.dma_start(offs_t[:], offs)
+        nc.sync.dma_start(ant_t[:], ant)
+
+        scale_win = keep.tile([P, T], U8, name="scale_win", align_bytes=64)
+        nc.gpsimd.memset(scale_win[:].bitcast(I32), 0)
+        rows = x_scales[0].rearrange("(q r) c -> r q c", r=4)
+        for r in range(4):
+            nc.sync.dma_start(scale_win[r:P:32, :].bitcast(I32), rows[r].bitcast(I32))
+
+        warm = keep.tile([P, 2], F32, name="warm")
+        nc.vector.memset(warm[:, 0:1], 0.0)
+        nc.scalar.activation(warm[:, 1:2], warm[:, 0:1], ACT.Exp)
+
+        word_win = keep.tile([P, T], I32, name="word_win", align_bytes=64)
+        nc.sync.dma_start(word_win[:], x_words[0].rearrange("p n t -> p (n t)").bitcast(I32))
+        w_rows = w1.rearrange("(p j) c -> p j c", j=PACK)
+        w_raw = [keep.tile([P, PACK, K // 2], F32, name="w_raw%d" % h) for h in range(2)]
+        for h in range(2):
+            nc.sync.dma_start(w_raw[h][:], w_rows[:, :, h * K // 2 : (h + 1) * K // 2])
+        ment_win = keep.tile([P, T], F32, name="ment_win")
+        nc.sync.dma_start(ment_win[:], ment)
+
+        span_scales = keep.tile([P, S], U8, name="span_scales", align_bytes=64)
+        ant_scales = keep.tile([P, V], U8, name="ant_scales", align_bytes=64)
+        span_words = keep.tile([P, S], U32, name="span_words", align_bytes=64)
+        ant_words = keep.tile([P, V], U32, name="ant_words", align_bytes=64)
+        nc.vector.tensor_copy(span_scales[:], scale_win[:].indirect(offs_t[:]))
+        nc.vector.tensor_copy(ant_scales[:], scale_win[:].indirect(ant_t[:]))
+        nc.vector.tensor_copy(span_words[:], word_win[:].bitcast(U32).indirect(offs_t[:]))
+        nc.vector.tensor_copy(ant_words[:], word_win[:].bitcast(U32).indirect(ant_t[:]))
+
+        w_bf = keep.tile([P, PACK, P, PACK], BF16, name="w_bf", align_bytes=64)
+        for h in range(2):
+            nc.scalar.copy(
+                w_bf[:, :, h * P // 2 : (h + 1) * P // 2, :].rearrange("p t m j -> p m t j"),
+                w_raw[h][:].rearrange("p j (m t) -> p m t j", t=PACK),
+            )
+        w_codes = keep.tile([P, K], U32, name="w_codes", align_bytes=64)
+        w_scales = keep.tile([P, K], U8, name="w_scales", align_bytes=64)
+        for h in range(2):
+            cols = slice(h * K // 2, (h + 1) * K // 2)
+            nc.vector.quantize_mx(
+                out=w_codes[:, cols].bitcast(FP8X4),
+                scales=w_scales[:, cols],
+                in_=w_bf[:, 2 * h : 2 * h + 2].rearrange("p t m j -> p (t m j)"),
+            )
+
+        ment_all = keep.tile([P, V], F32, name="ment_all")
+        nc.vector.tensor_copy(ment_all[:], ment_win[:].indirect(ant_t[:]))
+
+        z_bf = {}
+        y_neg = {}
+        y_ps = {}
+        low = {}
+
+        def first_product(i):
+            z_ps = psum.tile([P, PACK, P], F32, name="z_ps%d" % i, tag="bank")
+            for t in range(PACK):
+                nc.tensor.matmul_mx(
+                    out=z_ps[:, t, :],
+                    lhsT=w_codes[:, t * P : (t + 1) * P].bitcast(FP8X4),
+                    lhsT_scale=w_scales[:, t * P : (t + 1) * P],
+                    rhs=span_words[:, i * P : (i + 1) * P].bitcast(FP8X4),
+                    rhs_scale=span_scales[:, i * P : (i + 1) * P],
+                    start=True,
+                    stop=True,
+                )
+            z_bf[i] = keep.tile([P, P, PACK], BF16, name="z_bf%d" % i, align_bytes=64)
+            nc.scalar.copy(z_bf[i][:], z_ps[:].rearrange("p t n -> p n t"))
+
+        def second_product(i):
+            z_codes = keep.tile([P, P], U32, name="z_codes%d" % i, align_bytes=64)
+            z_scales = keep.tile([P, P], U8, name="z_scales%d" % i, align_bytes=64)
+            nc.vector.quantize_mx(
+                out=z_codes[:].bitcast(FP8X4), scales=z_scales[:], in_=z_bf[i][:].rearrange("p n t -> p (n t)")
+            )
+            y_ps[i] = psum.tile([P, V], F32, name="y_ps%d" % i, tag="bank")
+            nc.tensor.matmul_mx(
+                out=y_ps[i][:],
+                lhsT=z_codes[:].bitcast(FP8X4),
+                lhsT_scale=z_scales[:],
+                rhs=ant_words[:].bitcast(FP8X4),
+                rhs_scale=ant_scales[:],
+                start=True,
+                stop=True,
+            )
+
+        def scores(i):
+            y_neg[i] = keep.tile([P, V], F32, name="y_neg%d" % i)
+            nc.vector.scalar_tensor_tensor(y_neg[i][:], y_ps[i][:], -1.0, ment_all[:], ALU.mult, ALU.subtract)
+
+        def row_max(i):
+            low[i] = keep.tile([P, 1], F32, name="low%d" % i)
+            nc.vector.tensor_reduce(low[i][:], y_neg[i][:], mybir.AxisListType.X, ALU.min)
+
+        e = {}
+        total = {}
+
+        def exps(i):
+            e[i] = keep.tile([P, V], F32, name="e%d" % i)
+            total[i] = keep.tile([P, 1], F32, name="total%d" % i)
+            nc.scalar.activation(e[i][:], y_neg[i][:], ACT.Exp, bias=low[i][:], scale=-1.0, accum_out=total[i][:])
+
+        def finish(i):
+            inv = keep.tile([P, 1], F32, name="inv%d" % i)
+            nc.vector.reciprocal(inv[:], total[i][:])
+            res = keep.tile([P, V], F32, name="res%d" % i)
+            engine = nc.vector if i == TILES - 1 else nc.gpsimd
+            engine.tensor_scalar(res[:], e[i][:], inv[:], 0.0, ALU.mult, ALU.add)
+            nc.sync.dma_start(out[i * P : (i + 1) * P, :], res[:])
+
+        for i in range(TILES):
+            first_product(i)
+        second_product(0)
+        second_product(1)
+        for i in range(TILES):
+            scores(i)
+            if i + 2 < TILES:
+                second_product(i + 2)
+            row_max(i)
+            exps(i)
+            if i > 0:
+                finish(i - 1)
+        finish(TILES - 1)

@@ -42,30 +42,25 @@ def tile_picked_zcoref_soft_p_kernel(tc, x_words, x_scales, w1, ment, offs, ant,
         nc.vector.memset(warm[:, 0:1], 0.0)
         nc.scalar.activation(warm[:, 1:2], warm[:, 0:1], ACT.Exp)
 
+        w_raw = keep.tile([P, PACK, K], F32, name="w_raw")
+        nc.sync.dma_start(w_raw[:], w1.rearrange("(p j) c -> p j c", j=PACK))
         word_win = keep.tile([P, T], I32, name="word_win", align_bytes=64)
         nc.sync.dma_start(word_win[:], x_words[0].rearrange("p n t -> p (n t)").bitcast(I32))
-        w_rows = w1.rearrange("(p j) c -> p j c", j=PACK)
-        w_raw = [keep.tile([P, PACK, K // 2], F32, name="w_raw%d" % h) for h in range(2)]
-        for h in range(2):
-            nc.sync.dma_start(w_raw[h][:], w_rows[:, :, h * K // 2 : (h + 1) * K // 2])
         ment_win = keep.tile([P, T], F32, name="ment_win")
         nc.sync.dma_start(ment_win[:], ment)
 
         span_scales = keep.tile([P, S], U8, name="span_scales", align_bytes=64)
         ant_scales = keep.tile([P, V], U8, name="ant_scales", align_bytes=64)
-        span_words = keep.tile([P, S], U32, name="span_words", align_bytes=64)
+        span_words = [keep.tile([P, S // 2], U32, name="span_words%d" % h, align_bytes=64) for h in range(2)]
         ant_words = keep.tile([P, V], U32, name="ant_words", align_bytes=64)
         nc.vector.tensor_copy(span_scales[:], scale_win[:].indirect(offs_t[:]))
         nc.vector.tensor_copy(ant_scales[:], scale_win[:].indirect(ant_t[:]))
-        nc.vector.tensor_copy(span_words[:], word_win[:].bitcast(U32).indirect(offs_t[:]))
-        nc.vector.tensor_copy(ant_words[:], word_win[:].bitcast(U32).indirect(ant_t[:]))
 
         w_bf = keep.tile([P, PACK, P, PACK], BF16, name="w_bf", align_bytes=64)
-        for h in range(2):
-            nc.scalar.copy(
-                w_bf[:, :, h * P // 2 : (h + 1) * P // 2, :].rearrange("p t m j -> p m t j"),
-                w_raw[h][:].rearrange("p j (m t) -> p m t j", t=PACK),
-            )
+        w_to = w_bf[:].rearrange("p t m j -> p m t j")
+        w_from = w_raw[:].rearrange("p j (m t) -> p m t j", t=PACK)
+        nc.scalar.copy(w_to[:, : P // 2], w_from[:, : P // 2])
+        nc.vector.tensor_copy(w_to[:, P // 2 :], w_from[:, P // 2 :])
         w_codes = keep.tile([P, K], U32, name="w_codes", align_bytes=64)
         w_scales = keep.tile([P, K], U8, name="w_scales", align_bytes=64)
         for h in range(2):
@@ -76,8 +71,11 @@ def tile_picked_zcoref_soft_p_kernel(tc, x_words, x_scales, w1, ment, offs, ant,
                 in_=w_bf[:, 2 * h : 2 * h + 2].rearrange("p t m j -> p (t m j)"),
             )
 
+        half = S // 2 // GROUP
+        for h in range(2):
+            nc.vector.tensor_copy(span_words[h][:], word_win[:].bitcast(U32).indirect(offs_t[:, h * half : (h + 1) * half]))
+        nc.vector.tensor_copy(ant_words[:], word_win[:].bitcast(U32).indirect(ant_t[:]))
         ment_all = keep.tile([P, V], F32, name="ment_all")
-        nc.vector.tensor_copy(ment_all[:], ment_win[:].indirect(ant_t[:]))
 
         z_bf = {}
         y_neg = {}
@@ -91,7 +89,7 @@ def tile_picked_zcoref_soft_p_kernel(tc, x_words, x_scales, w1, ment, offs, ant,
                     out=z_ps[:, t, :],
                     lhsT=w_codes[:, t * P : (t + 1) * P].bitcast(FP8X4),
                     lhsT_scale=w_scales[:, t * P : (t + 1) * P],
-                    rhs=span_words[:, i * P : (i + 1) * P].bitcast(FP8X4),
+                    rhs=span_words[i // 2][:, i % 2 * P : (i % 2 + 1) * P].bitcast(FP8X4),
                     rhs_scale=span_scales[:, i * P : (i + 1) * P],
                     start=True,
                     stop=True,
@@ -118,10 +116,15 @@ def tile_picked_zcoref_soft_p_kernel(tc, x_words, x_scales, w1, ment, offs, ant,
 
         def scores(i):
             y_neg[i] = keep.tile([P, V], F32, name="y_neg%d" % i)
-            nc.vector.scalar_tensor_tensor(y_neg[i][:], y_ps[i][:], -1.0, ment_all[:], ALU.mult, ALU.subtract)
+            if i == 1:
+                staged = keep.tile([P, V], F32, name="staged")
+                nc.scalar.activation(staged[:], y_ps[i][:], ACT.Copy, scale=-1.0)
+                nc.gpsimd.tensor_tensor(y_neg[i][:], staged[:], ment_all[:], ALU.subtract)
+            else:
+                nc.vector.scalar_tensor_tensor(y_neg[i][:], y_ps[i][:], -1.0, ment_all[:], ALU.mult, ALU.subtract)
 
         def row_max(i):
-            low[i] = keep.tile([P, 1], F32, name="low%d" % i)
+            low[i] = keep.tile([P, 1], F32, name="low%d" % i, tag="total0" if i == 1 else "low%d" % i)
             nc.vector.tensor_reduce(low[i][:], y_neg[i][:], mybir.AxisListType.X, ALU.min)
 
         e = {}
@@ -129,27 +132,37 @@ def tile_picked_zcoref_soft_p_kernel(tc, x_words, x_scales, w1, ment, offs, ant,
 
         def exps(i):
             e[i] = keep.tile([P, V], F32, name="e%d" % i)
-            total[i] = keep.tile([P, 1], F32, name="total%d" % i)
+            total[i] = keep.tile([P, 1], F32, name="total%d" % i, tag="total%d" % i)
             nc.scalar.activation(e[i][:], y_neg[i][:], ACT.Exp, bias=low[i][:], scale=-1.0, accum_out=total[i][:])
 
         def finish(i):
             inv = keep.tile([P, 1], F32, name="inv%d" % i)
             nc.vector.reciprocal(inv[:], total[i][:])
             res = keep.tile([P, V], F32, name="res%d" % i)
-            engine = nc.vector if i == TILES - 1 else nc.gpsimd
-            engine.tensor_scalar(res[:], e[i][:], inv[:], 0.0, ALU.mult, ALU.add)
+            if i == 0:
+                nc.gpsimd.tensor_scalar(res[:], e[i][:], inv[:], 0.0, ALU.mult, ALU.add)
+            else:
+                nc.vector.tensor_scalar(res[:], e[i][:], inv[:], None, ALU.mult)
             nc.sync.dma_start(out[i * P : (i + 1) * P, :], res[:])
 
         for i in range(TILES):
             first_product(i)
         second_product(0)
         second_product(1)
-        for i in range(TILES):
-            scores(i)
-            if i + 2 < TILES:
-                second_product(i + 2)
+        nc.vector.tensor_copy(ment_all[:], ment_win[:].indirect(ant_t[:]))
+        second_product(2)
+        second_product(3)
+        scores(0)
+        scores(1)
+        scores(2)
+        row_max(0)
+        exps(0)
+        finish(0)
+        scores(3)
+        row_max(2)
+        exps(2)
+        for i in (1, 3):
             row_max(i)
             exps(i)
-            if i > 0:
-                finish(i - 1)
-        finish(TILES - 1)
+        for i in (2, 1, 3):
+            finish(i)

@@ -42,25 +42,30 @@ def tile_picked_zcoref_soft_p_kernel(tc, x_words, x_scales, w1, ment, offs, ant,
         nc.vector.memset(warm[:, 0:1], 0.0)
         nc.scalar.activation(warm[:, 1:2], warm[:, 0:1], ACT.Exp)
 
-        w_raw = keep.tile([P, PACK, K], F32, name="w_raw")
-        nc.sync.dma_start(w_raw[:], w1.rearrange("(p j) c -> p j c", j=PACK))
         word_win = keep.tile([P, T], I32, name="word_win", align_bytes=64)
         nc.sync.dma_start(word_win[:], x_words[0].rearrange("p n t -> p (n t)").bitcast(I32))
+        w_rows = w1.rearrange("(p j) c -> p j c", j=PACK)
+        w_raw = [keep.tile([P, PACK, K // 2], F32, name="w_raw%d" % h) for h in range(2)]
+        for h in range(2):
+            nc.sync.dma_start(w_raw[h][:], w_rows[:, :, h * K // 2 : (h + 1) * K // 2])
         ment_win = keep.tile([P, T], F32, name="ment_win")
         nc.sync.dma_start(ment_win[:], ment)
 
         span_scales = keep.tile([P, S], U8, name="span_scales", align_bytes=64)
         ant_scales = keep.tile([P, V], U8, name="ant_scales", align_bytes=64)
-        span_words = [keep.tile([P, S // 2], U32, name="span_words%d" % h, align_bytes=64) for h in range(2)]
+        span_words = keep.tile([P, S], U32, name="span_words", align_bytes=64)
         ant_words = keep.tile([P, V], U32, name="ant_words", align_bytes=64)
         nc.vector.tensor_copy(span_scales[:], scale_win[:].indirect(offs_t[:]))
         nc.vector.tensor_copy(ant_scales[:], scale_win[:].indirect(ant_t[:]))
+        nc.vector.tensor_copy(span_words[:], word_win[:].bitcast(U32).indirect(offs_t[:]))
+        nc.vector.tensor_copy(ant_words[:], word_win[:].bitcast(U32).indirect(ant_t[:]))
 
         w_bf = keep.tile([P, PACK, P, PACK], BF16, name="w_bf", align_bytes=64)
         w_to = w_bf[:].rearrange("p t m j -> p m t j")
-        w_from = w_raw[:].rearrange("p j (m t) -> p m t j", t=PACK)
-        nc.scalar.copy(w_to[:, : P // 2], w_from[:, : P // 2])
-        nc.vector.tensor_copy(w_to[:, P // 2 :], w_from[:, P // 2 :])
+        w_from = [raw[:].rearrange("p j (m t) -> p m t j", t=PACK) for raw in w_raw]
+        nc.scalar.copy(w_to[:, :64], w_from[0])
+        nc.scalar.copy(w_to[:, 64:96], w_from[1][:, :32])
+        nc.vector.tensor_copy(w_to[:, 96:], w_from[1][:, 32:])
         w_codes = keep.tile([P, K], U32, name="w_codes", align_bytes=64)
         w_scales = keep.tile([P, K], U8, name="w_scales", align_bytes=64)
         for h in range(2):
@@ -71,10 +76,6 @@ def tile_picked_zcoref_soft_p_kernel(tc, x_words, x_scales, w1, ment, offs, ant,
                 in_=w_bf[:, 2 * h : 2 * h + 2].rearrange("p t m j -> p (t m j)"),
             )
 
-        half = S // 2 // GROUP
-        for h in range(2):
-            nc.vector.tensor_copy(span_words[h][:], word_win[:].bitcast(U32).indirect(offs_t[:, h * half : (h + 1) * half]))
-        nc.vector.tensor_copy(ant_words[:], word_win[:].bitcast(U32).indirect(ant_t[:]))
         ment_all = keep.tile([P, V], F32, name="ment_all")
 
         z_bf = {}
@@ -89,7 +90,7 @@ def tile_picked_zcoref_soft_p_kernel(tc, x_words, x_scales, w1, ment, offs, ant,
                     out=z_ps[:, t, :],
                     lhsT=w_codes[:, t * P : (t + 1) * P].bitcast(FP8X4),
                     lhsT_scale=w_scales[:, t * P : (t + 1) * P],
-                    rhs=span_words[i // 2][:, i % 2 * P : (i % 2 + 1) * P].bitcast(FP8X4),
+                    rhs=span_words[:, i * P : (i + 1) * P].bitcast(FP8X4),
                     rhs_scale=span_scales[:, i * P : (i + 1) * P],
                     start=True,
                     stop=True,
@@ -135,9 +136,14 @@ def tile_picked_zcoref_soft_p_kernel(tc, x_words, x_scales, w1, ment, offs, ant,
             total[i] = keep.tile([P, 1], F32, name="total%d" % i, tag="total%d" % i)
             nc.scalar.activation(e[i][:], y_neg[i][:], ACT.Exp, bias=low[i][:], scale=-1.0, accum_out=total[i][:])
 
+        invs = {}
+
+        def invert(i):
+            invs[i] = keep.tile([P, 1], F32, name="inv%d" % i)
+            nc.vector.reciprocal(invs[i][:], total[i][:])
+
         def finish(i):
-            inv = keep.tile([P, 1], F32, name="inv%d" % i)
-            nc.vector.reciprocal(inv[:], total[i][:])
+            inv = invs[i]
             res = keep.tile([P, V], F32, name="res%d" % i)
             if i == 0:
                 nc.gpsimd.tensor_scalar(res[:], e[i][:], inv[:], 0.0, ALU.mult, ALU.add)
@@ -157,6 +163,7 @@ def tile_picked_zcoref_soft_p_kernel(tc, x_words, x_scales, w1, ment, offs, ant,
         scores(2)
         row_max(0)
         exps(0)
+        invert(0)
         finish(0)
         scores(3)
         row_max(2)
@@ -164,5 +171,9 @@ def tile_picked_zcoref_soft_p_kernel(tc, x_words, x_scales, w1, ment, offs, ant,
         for i in (1, 3):
             row_max(i)
             exps(i)
-        for i in (2, 1, 3):
-            finish(i)
+        invert(2)
+        invert(1)
+        finish(2)
+        finish(1)
+        invert(3)
+        finish(3)

@@ -19,6 +19,7 @@ P = 128
 PACK = 4
 GROUP = 16
 TILES = S // P
+HEAD = 768
 
 
 def tile_picked_zcoref_soft_p_kernel(tc, x_words, x_scales, w1, ment, offs, ant, out):
@@ -27,6 +28,9 @@ def tile_picked_zcoref_soft_p_kernel(tc, x_words, x_scales, w1, ment, offs, ant,
         keep = ctx.enter_context(tc.tile_pool(name="keep", bufs=1))
         psum = ctx.enter_context(tc.psum_pool(name="psum", bufs=8))
 
+        word_win = keep.tile([P, T], I32, name="word_win", align_bytes=64)
+        words = x_words[0].rearrange("p n t -> p (n t)").bitcast(I32)
+        nc.sync.dma_start(word_win[:, :HEAD], words[:, :HEAD])
         offs_t = keep.tile([P, S // GROUP], U16, name="offs_t")
         ant_t = keep.tile([P, V // GROUP], U16, name="ant_t")
         nc.sync.dma_start(offs_t[:], offs)
@@ -42,8 +46,7 @@ def tile_picked_zcoref_soft_p_kernel(tc, x_words, x_scales, w1, ment, offs, ant,
         nc.vector.memset(warm[:, 0:1], 0.0)
         nc.scalar.activation(warm[:, 1:2], warm[:, 0:1], ACT.Exp)
 
-        word_win = keep.tile([P, T], I32, name="word_win", align_bytes=64)
-        nc.sync.dma_start(word_win[:], x_words[0].rearrange("p n t -> p (n t)").bitcast(I32))
+        nc.sync.dma_start(word_win[:, HEAD:], words[:, HEAD:])
         w_rows = w1.rearrange("(p j) c -> p j c", j=PACK)
         w_raw = [keep.tile([P, PACK, K // 2], F32, name="w_raw%d" % h) for h in range(2)]
         for h in range(2):
@@ -64,8 +67,8 @@ def tile_picked_zcoref_soft_p_kernel(tc, x_words, x_scales, w1, ment, offs, ant,
         w_to = w_bf[:].rearrange("p t m j -> p m t j")
         w_from = [raw[:].rearrange("p j (m t) -> p m t j", t=PACK) for raw in w_raw]
         nc.scalar.copy(w_to[:, :64], w_from[0])
-        nc.scalar.copy(w_to[:, 64:96], w_from[1][:, :32])
-        nc.vector.tensor_copy(w_to[:, 96:], w_from[1][:, 32:])
+        nc.scalar.copy(w_to[:, 64:112], w_from[1][:, :48])
+        nc.vector.tensor_copy(w_to[:, 112:], w_from[1][:, 48:])
         w_codes = keep.tile([P, K], U32, name="w_codes", align_bytes=64)
         w_scales = keep.tile([P, K], U8, name="w_scales", align_bytes=64)
         for h in range(2):

@@ -63,6 +63,18 @@ def tile_picked_zcoref_soft_p_kernel(tc, x_words, x_scales, w1, ment, offs, ant,
         nc.vector.tensor_copy(span_words[:], word_win[:].bitcast(U32).indirect(offs_t[:]))
         nc.vector.tensor_copy(ant_words[:], word_win[:].bitcast(U32).indirect(ant_t[:]))
 
+        idle = psum.tile([P, S], F32, name="idle", tag="bank")
+        for c in range(2):
+            nc.tensor.matmul_mx(
+                out=idle[:],
+                lhsT=span_words[:, :P].bitcast(FP8X4),
+                lhsT_scale=span_scales[:, :P],
+                rhs=span_words[:].bitcast(FP8X4),
+                rhs_scale=span_scales[:],
+                start=True,
+                stop=True,
+            )
+
         w_bf = keep.tile([P, PACK, P, PACK], BF16, name="w_bf", align_bytes=64)
         w_to = w_bf[:].rearrange("p t m j -> p m t j")
         w_from = [raw[:].rearrange("p j (m t) -> p m t j", t=PACK) for raw in w_raw]

@@ -1,6 +1,7 @@
 from contextlib import ExitStack
 
 import concourse.mybir as mybir
+from concourse.masks import make_identity
 
 K, T, S, V = 512, 2048, 512, 512
 FLOPS = 2 * K * K * S + 2 * K * S * V
@@ -19,7 +20,8 @@ P = 128
 PACK = 4
 GROUP = 16
 TILES = S // P
-HEAD = 768
+CUT = 96
+ROW = 127
 
 
 def tile_picked_zcoref_soft_p_kernel(tc, x_words, x_scales, w1, ment, offs, ant, out):
@@ -28,13 +30,17 @@ def tile_picked_zcoref_soft_p_kernel(tc, x_words, x_scales, w1, ment, offs, ant,
         keep = ctx.enter_context(tc.tile_pool(name="keep", bufs=1))
         psum = ctx.enter_context(tc.psum_pool(name="psum", bufs=8))
 
-        word_win = keep.tile([P, T], I32, name="word_win", align_bytes=64)
-        words = x_words[0].rearrange("p n t -> p (n t)").bitcast(I32)
-        nc.sync.dma_start(word_win[:, :HEAD], words[:, :HEAD])
         offs_t = keep.tile([P, S // GROUP], U16, name="offs_t")
         ant_t = keep.tile([P, V // GROUP], U16, name="ant_t")
-        nc.sync.dma_start(offs_t[:], offs)
+        ment_win = keep.tile([P, T], F32, name="ment_win")
+        nc.vector.memset(ment_win[:ROW, :], 0.0)
         nc.sync.dma_start(ant_t[:], ant)
+        nc.sync.dma_start(ment_win[ROW:, :], ment[ROW:, :])
+        w_rows = w1.rearrange("(p j) c -> p j c", j=PACK)
+        w_raw = keep.tile([P, PACK, CUT * PACK], F32, name="w_raw")
+        w_end = keep.tile([P, PACK, K - CUT * PACK], F32, name="w_end")
+        nc.sync.dma_start(w_raw[:], w_rows[:, :, : CUT * PACK])
+        nc.sync.dma_start(offs_t[:], offs)
 
         scale_win = keep.tile([P, T], U8, name="scale_win", align_bytes=64)
         nc.gpsimd.memset(scale_win[:].bitcast(I32), 0)
@@ -42,61 +48,60 @@ def tile_picked_zcoref_soft_p_kernel(tc, x_words, x_scales, w1, ment, offs, ant,
         for r in range(4):
             nc.sync.dma_start(scale_win[r:P:32, :].bitcast(I32), rows[r].bitcast(I32))
 
-        warm = keep.tile([P, 2], F32, name="warm")
-        nc.vector.memset(warm[:, 0:1], 0.0)
-        nc.scalar.activation(warm[:, 1:2], warm[:, 0:1], ACT.Exp)
+        nc.sync.dma_start(w_end[:], w_rows[:, :, CUT * PACK :])
+        word_win = keep.tile([P, T], I32, name="word_win", align_bytes=64)
+        nc.sync.dma_start(word_win[:], x_words[0].rearrange("p n t -> p (n t)").bitcast(I32))
 
-        nc.sync.dma_start(word_win[:, HEAD:], words[:, HEAD:])
-        w_rows = w1.rearrange("(p j) c -> p j c", j=PACK)
-        w_raw = [keep.tile([P, PACK, K // 2], F32, name="w_raw%d" % h) for h in range(2)]
-        for h in range(2):
-            nc.sync.dma_start(w_raw[h][:], w_rows[:, :, h * K // 2 : (h + 1) * K // 2])
-        ment_win = keep.tile([P, T], F32, name="ment_win")
-        nc.sync.dma_start(ment_win[:], ment)
+        ident = keep.tile([P, P], F32, name="ident")
+        make_identity(nc, ident[:])
+        warm = keep.tile([P, 1], F32, name="warm")
+        nc.scalar.activation(warm[:], ident[:, 0:1], ACT.Exp)
+
+        ment_row = keep.tile([P, V], F32, name="ment_row")
+        nc.vector.tensor_copy(ment_row[:], ment_win[:].indirect(ant_t[:]))
+        turned = psum.tile([P, TILES, P], F32, name="turned", tag="bank")
+        for c in range(TILES):
+            nc.tensor.transpose(turned[:, c, :], ment_row[:, c * P : (c + 1) * P], ident[:])
+        ment_col = keep.tile([P, TILES], F32, name="ment_col")
+        nc.scalar.copy(ment_col[:], turned[:, :, ROW])
+        spread = psum.tile([P, TILES, P], F32, name="spread", tag="bank")
+        for c in range(TILES):
+            nc.tensor.transpose(spread[:, c, :], ment_col[:, c : c + 1].to_broadcast([P, P]), ident[:])
 
         span_scales = keep.tile([P, S], U8, name="span_scales", align_bytes=64)
         ant_scales = keep.tile([P, V], U8, name="ant_scales", align_bytes=64)
-        span_words = keep.tile([P, S], U32, name="span_words", align_bytes=64)
+        span_words = [keep.tile([P, S // 2], U32, name="span_words%d" % h, align_bytes=64) for h in range(2)]
         ant_words = keep.tile([P, V], U32, name="ant_words", align_bytes=64)
         nc.vector.tensor_copy(span_scales[:], scale_win[:].indirect(offs_t[:]))
         nc.vector.tensor_copy(ant_scales[:], scale_win[:].indirect(ant_t[:]))
-        nc.vector.tensor_copy(span_words[:], word_win[:].bitcast(U32).indirect(offs_t[:]))
-        nc.vector.tensor_copy(ant_words[:], word_win[:].bitcast(U32).indirect(ant_t[:]))
-
-        idle = psum.tile([P, S], F32, name="idle", tag="bank")
-        for c in range(2):
-            nc.tensor.matmul_mx(
-                out=idle[:],
-                lhsT=span_words[:, :P].bitcast(FP8X4),
-                lhsT_scale=span_scales[:, :P],
-                rhs=span_words[:].bitcast(FP8X4),
-                rhs_scale=span_scales[:],
-                start=True,
-                stop=True,
-            )
 
         w_bf = keep.tile([P, PACK, P, PACK], BF16, name="w_bf", align_bytes=64)
         w_to = w_bf[:].rearrange("p t m j -> p m t j")
-        w_from = [raw[:].rearrange("p j (m t) -> p m t j", t=PACK) for raw in w_raw]
-        nc.scalar.copy(w_to[:, :64], w_from[0])
-        nc.scalar.copy(w_to[:, 64:112], w_from[1][:, :48])
-        nc.vector.tensor_copy(w_to[:, 112:], w_from[1][:, 48:])
+        nc.scalar.copy(w_to[:, :CUT], w_raw[:].rearrange("p j (m t) -> p m t j", t=PACK))
+        nc.scalar.copy(w_to[:, CUT:], w_end[:].rearrange("p j (m t) -> p m t j", t=PACK))
         w_codes = keep.tile([P, K], U32, name="w_codes", align_bytes=64)
         w_scales = keep.tile([P, K], U8, name="w_scales", align_bytes=64)
-        for h in range(2):
-            cols = slice(h * K // 2, (h + 1) * K // 2)
-            nc.vector.quantize_mx(
-                out=w_codes[:, cols].bitcast(FP8X4),
-                scales=w_scales[:, cols],
-                in_=w_bf[:, 2 * h : 2 * h + 2].rearrange("p t m j -> p (t m j)"),
-            )
+        nc.vector.quantize_mx(
+            out=w_codes[:].bitcast(FP8X4), scales=w_scales[:], in_=w_bf[:].rearrange("p t m j -> p (t m j)")
+        )
 
-        ment_all = keep.tile([P, V], F32, name="ment_all")
+        ment_all = w_end[:].rearrange("p j c -> p (j c)")
+        nc.scalar.copy(ment_all, spread[:].rearrange("p c n -> p (c n)"))
+
+        half = S // GROUP // 2
+        for h in range(2):
+            nc.vector.tensor_copy(
+                span_words[h][:], word_win[:].bitcast(U32).indirect(offs_t[:, h * half : (h + 1) * half])
+            )
+        nc.vector.tensor_copy(ant_words[:], word_win[:].bitcast(U32).indirect(ant_t[:]))
 
         z_bf = {}
         y_neg = {}
         y_ps = {}
         low = {}
+        e = {}
+        total = {}
+        invs = {}
 
         def first_product(i):
             z_ps = psum.tile([P, PACK, P], F32, name="z_ps%d" % i, tag="bank")
@@ -105,7 +110,7 @@ def tile_picked_zcoref_soft_p_kernel(tc, x_words, x_scales, w1, ment, offs, ant,
                     out=z_ps[:, t, :],
                     lhsT=w_codes[:, t * P : (t + 1) * P].bitcast(FP8X4),
                     lhsT_scale=w_scales[:, t * P : (t + 1) * P],
-                    rhs=span_words[:, i * P : (i + 1) * P].bitcast(FP8X4),
+                    rhs=span_words[i // 2][:, (i % 2) * P : (i % 2 + 1) * P].bitcast(FP8X4),
                     rhs_scale=span_scales[:, i * P : (i + 1) * P],
                     start=True,
                     stop=True,
@@ -130,65 +135,51 @@ def tile_picked_zcoref_soft_p_kernel(tc, x_words, x_scales, w1, ment, offs, ant,
                 stop=True,
             )
 
-        def scores(i):
+        def scores_direct(i):
             y_neg[i] = keep.tile([P, V], F32, name="y_neg%d" % i)
-            if i == 1:
-                staged = keep.tile([P, V], F32, name="staged")
-                nc.scalar.activation(staged[:], y_ps[i][:], ACT.Copy, scale=-1.0)
-                nc.gpsimd.tensor_tensor(y_neg[i][:], staged[:], ment_all[:], ALU.subtract)
-            else:
-                nc.vector.scalar_tensor_tensor(y_neg[i][:], y_ps[i][:], -1.0, ment_all[:], ALU.mult, ALU.subtract)
+            nc.vector.scalar_tensor_tensor(y_neg[i][:], y_ps[i][:], -1.0, ment_all, ALU.mult, ALU.subtract)
+
+        def scores_staged(i):
+            y_neg[i] = keep.tile([P, V], F32, name="y_neg%d" % i)
+            staged = keep.tile([P, V], F32, name="staged%d" % i)
+            nc.scalar.activation(staged[:], y_ps[i][:], ACT.Copy, scale=-1.0)
+            nc.gpsimd.tensor_tensor(y_neg[i][:], staged[:], ment_all, ALU.subtract)
 
         def row_max(i):
-            low[i] = keep.tile([P, 1], F32, name="low%d" % i, tag="total0" if i == 1 else "low%d" % i)
+            low[i] = keep.tile([P, 1], F32, name="low%d" % i)
             nc.vector.tensor_reduce(low[i][:], y_neg[i][:], mybir.AxisListType.X, ALU.min)
-
-        e = {}
-        total = {}
 
         def exps(i):
             e[i] = keep.tile([P, V], F32, name="e%d" % i)
-            total[i] = keep.tile([P, 1], F32, name="total%d" % i, tag="total%d" % i)
+            total[i] = keep.tile([P, 1], F32, name="total%d" % i)
             nc.scalar.activation(e[i][:], y_neg[i][:], ACT.Exp, bias=low[i][:], scale=-1.0, accum_out=total[i][:])
-
-        invs = {}
 
         def invert(i):
             invs[i] = keep.tile([P, 1], F32, name="inv%d" % i)
             nc.vector.reciprocal(invs[i][:], total[i][:])
 
-        def finish(i):
-            inv = invs[i]
+        def finish(i, on_vector):
             res = keep.tile([P, V], F32, name="res%d" % i)
-            if i == 0:
-                nc.gpsimd.tensor_scalar(res[:], e[i][:], inv[:], 0.0, ALU.mult, ALU.add)
+            if on_vector:
+                nc.vector.tensor_scalar(res[:], e[i][:], invs[i][:], None, ALU.mult)
             else:
-                nc.vector.tensor_scalar(res[:], e[i][:], inv[:], None, ALU.mult)
+                nc.gpsimd.tensor_scalar(res[:], e[i][:], invs[i][:], 0.0, ALU.mult, ALU.add)
             nc.sync.dma_start(out[i * P : (i + 1) * P, :], res[:])
 
         for i in range(TILES):
             first_product(i)
-        second_product(0)
-        second_product(1)
-        nc.vector.tensor_copy(ment_all[:], ment_win[:].indirect(ant_t[:]))
-        second_product(2)
-        second_product(3)
-        scores(0)
-        scores(1)
-        scores(2)
+        for i in range(TILES):
+            second_product(i)
+        scores_direct(0)
+        scores_staged(1)
         row_max(0)
         exps(0)
         invert(0)
-        finish(0)
-        scores(3)
-        row_max(2)
-        exps(2)
-        for i in (1, 3):
+        finish(0, False)
+        scores_direct(2)
+        scores_direct(3)
+        for i in (2, 1, 3):
             row_max(i)
             exps(i)
-        invert(2)
-        invert(1)
-        finish(2)
-        finish(1)
-        invert(3)
-        finish(3)
+            invert(i)
+            finish(i, i != 2)

@@ -22,6 +22,7 @@ GROUP = 16
 TILES = S // P
 CUT = 96
 ROW = 127
+HOLD = {1: "total0"}
 
 
 def tile_picked_zcoref_soft_p_kernel(tc, x_words, x_scales, w1, ment, offs, ant, out):
@@ -81,9 +82,24 @@ def tile_picked_zcoref_soft_p_kernel(tc, x_words, x_scales, w1, ment, offs, ant,
         nc.scalar.copy(w_to[:, CUT:], w_end[:].rearrange("p j (m t) -> p m t j", t=PACK))
         w_codes = keep.tile([P, K], U32, name="w_codes", align_bytes=64)
         w_scales = keep.tile([P, K], U8, name="w_scales", align_bytes=64)
-        nc.vector.quantize_mx(
-            out=w_codes[:].bitcast(FP8X4), scales=w_scales[:], in_=w_bf[:].rearrange("p t m j -> p (t m j)")
-        )
+        for h in range(2):
+            cols = slice(h * K // 2, (h + 1) * K // 2)
+            nc.vector.quantize_mx(
+                out=w_codes[:, cols].bitcast(FP8X4),
+                scales=w_scales[:, cols],
+                in_=w_bf[:, 2 * h : 2 * h + 2].rearrange("p t m j -> p (t m j)"),
+            )
+        idle = psum.tile([P, K // 2], F32, name="idle", tag="bank")
+        for c in range(4):
+            nc.tensor.matmul_mx(
+                out=idle[:],
+                lhsT=w_codes[:, :P].bitcast(FP8X4),
+                lhsT_scale=w_scales[:, :P],
+                rhs=w_codes[:, : K // 2].bitcast(FP8X4),
+                rhs_scale=w_scales[:, : K // 2],
+                start=True,
+                stop=True,
+            )
 
         ment_all = w_end[:].rearrange("p j c -> p (j c)")
         nc.scalar.copy(ment_all, spread[:].rearrange("p c n -> p (c n)"))
@@ -146,22 +162,24 @@ def tile_picked_zcoref_soft_p_kernel(tc, x_words, x_scales, w1, ment, offs, ant,
             nc.gpsimd.tensor_tensor(y_neg[i][:], staged[:], ment_all, ALU.subtract)
 
         def row_max(i):
-            low[i] = keep.tile([P, 1], F32, name="low%d" % i)
+            low[i] = keep.tile([P, 1], F32, name="low%d" % i, tag=HOLD.get(i, "low%d" % i))
             nc.vector.tensor_reduce(low[i][:], y_neg[i][:], mybir.AxisListType.X, ALU.min)
 
         def exps(i):
             e[i] = keep.tile([P, V], F32, name="e%d" % i)
-            total[i] = keep.tile([P, 1], F32, name="total%d" % i)
+            total[i] = keep.tile([P, 1], F32, name="total%d" % i, tag="total%d" % i)
             nc.scalar.activation(e[i][:], y_neg[i][:], ACT.Exp, bias=low[i][:], scale=-1.0, accum_out=total[i][:])
 
         def invert(i):
-            invs[i] = keep.tile([P, 1], F32, name="inv%d" % i)
+            invs[i] = keep.tile([P, 1], F32, name="inv%d" % i, tag="inv%d" % i)
             nc.vector.reciprocal(invs[i][:], total[i][:])
 
-        def finish(i, on_vector):
+        def finish(i, engine):
             res = keep.tile([P, V], F32, name="res%d" % i)
-            if on_vector:
+            if engine == "vector":
                 nc.vector.tensor_scalar(res[:], e[i][:], invs[i][:], None, ALU.mult)
+            elif engine == "scalar":
+                nc.scalar.activation(res[:], e[i][:], ACT.Copy, scale=invs[i][:])
             else:
                 nc.gpsimd.tensor_scalar(res[:], e[i][:], invs[i][:], 0.0, ALU.mult, ALU.add)
             nc.sync.dma_start(out[i * P : (i + 1) * P, :], res[:])
@@ -172,14 +190,20 @@ def tile_picked_zcoref_soft_p_kernel(tc, x_words, x_scales, w1, ment, offs, ant,
             second_product(i)
         scores_direct(0)
         scores_staged(1)
+        scores_direct(2)
         row_max(0)
         exps(0)
         invert(0)
-        finish(0, False)
-        scores_direct(2)
+        finish(0, "gpsimd")
         scores_direct(3)
-        for i in (2, 1, 3):
+        row_max(2)
+        exps(2)
+        for i in (1, 3):
             row_max(i)
             exps(i)
-            invert(i)
-            finish(i, i != 2)
+        invert(2)
+        invert(1)
+        finish(2, "vector")
+        finish(1, "vector")
+        invert(3)
+        finish(3, "vector")

@@ -20,9 +20,11 @@ P = 128
 PACK = 4
 GROUP = 16
 TILES = S // P
-CUT = 96
+CUT = 80
 ROW = 127
-HOLD = {1: "total0"}
+CLEAR = 1536
+TURNED = (1, 2)
+HOLD = {0: "z_bf3", 2: "total0"}
 
 
 def tile_picked_zcoref_soft_p_kernel(tc, x_words, x_scales, w1, ment, offs, ant, out):
@@ -34,7 +36,10 @@ def tile_picked_zcoref_soft_p_kernel(tc, x_words, x_scales, w1, ment, offs, ant,
         offs_t = keep.tile([P, S // GROUP], U16, name="offs_t")
         ant_t = keep.tile([P, V // GROUP], U16, name="ant_t")
         ment_win = keep.tile([P, T], F32, name="ment_win")
-        nc.vector.memset(ment_win[:ROW, :], 0.0)
+        warm = keep.tile([P, 2], F32, name="warm")
+        nc.vector.memset(warm[:, 0:1], 0.0)
+        nc.scalar.activation(warm[:, 1:2], warm[:, 0:1], ACT.Exp)
+        nc.vector.memset(ment_win[:ROW, :CLEAR], 0.0)
         nc.sync.dma_start(ant_t[:], ant)
         nc.sync.dma_start(ment_win[ROW:, :], ment[ROW:, :])
         w_rows = w1.rearrange("(p j) c -> p j c", j=PACK)
@@ -55,8 +60,7 @@ def tile_picked_zcoref_soft_p_kernel(tc, x_words, x_scales, w1, ment, offs, ant,
 
         ident = keep.tile([P, P], F32, name="ident")
         make_identity(nc, ident[:])
-        warm = keep.tile([P, 1], F32, name="warm")
-        nc.scalar.activation(warm[:], ident[:, 0:1], ACT.Exp)
+        nc.gpsimd.memset(ment_win[:ROW, CLEAR:], 0.0)
 
         ment_row = keep.tile([P, V], F32, name="ment_row")
         nc.vector.tensor_copy(ment_row[:], ment_win[:].indirect(ant_t[:]))
@@ -64,10 +68,22 @@ def tile_picked_zcoref_soft_p_kernel(tc, x_words, x_scales, w1, ment, offs, ant,
         for c in range(TILES):
             nc.tensor.transpose(turned[:, c, :], ment_row[:, c * P : (c + 1) * P], ident[:])
         ment_col = keep.tile([P, TILES], F32, name="ment_col")
-        nc.scalar.copy(ment_col[:], turned[:, :, ROW])
+        nc.scalar.activation(ment_col[:], turned[:, :, ROW], ACT.Copy, scale=-1.0)
         spread = psum.tile([P, TILES, P], F32, name="spread", tag="bank")
         for c in range(TILES):
             nc.tensor.transpose(spread[:, c, :], ment_col[:, c : c + 1].to_broadcast([P, P]), ident[:])
+        y_neg = {}
+        for i in TURNED:
+            y_neg[i] = psum.tile([P, V], F32, name="y_neg%d" % i, tag="bank")
+            for c in range(TILES):
+                nc.tensor.matmul(
+                    y_neg[i][:, c * P : (c + 1) * P],
+                    ment_col[:, c : c + 1].to_broadcast([P, P]),
+                    ident[:],
+                    start=c == 0,
+                    stop=False,
+                    is_transpose=True,
+                )
 
         span_scales = keep.tile([P, S], U8, name="span_scales", align_bytes=64)
         ant_scales = keep.tile([P, V], U8, name="ant_scales", align_bytes=64)
@@ -101,7 +117,7 @@ def tile_picked_zcoref_soft_p_kernel(tc, x_words, x_scales, w1, ment, offs, ant,
                 stop=True,
             )
 
-        ment_all = w_end[:].rearrange("p j c -> p (j c)")
+        ment_all = w_end[:].rearrange("p j c -> p (j c)")[:, :V]
         nc.scalar.copy(ment_all, spread[:].rearrange("p c n -> p (c n)"))
 
         half = S // GROUP // 2
@@ -112,7 +128,6 @@ def tile_picked_zcoref_soft_p_kernel(tc, x_words, x_scales, w1, ment, offs, ant,
         nc.vector.tensor_copy(ant_words[:], word_win[:].bitcast(U32).indirect(ant_t[:]))
 
         z_bf = {}
-        y_neg = {}
         y_ps = {}
         low = {}
         e = {}
@@ -131,7 +146,7 @@ def tile_picked_zcoref_soft_p_kernel(tc, x_words, x_scales, w1, ment, offs, ant,
                     start=True,
                     stop=True,
                 )
-            z_bf[i] = keep.tile([P, P, PACK], BF16, name="z_bf%d" % i, align_bytes=64)
+            z_bf[i] = keep.tile([P, P, PACK], BF16, name="z_bf%d" % i, tag="z_bf%d" % i, align_bytes=64)
             nc.scalar.copy(z_bf[i][:], z_ps[:].rearrange("p t n -> p n t"))
 
         def second_product(i):
@@ -141,6 +156,18 @@ def tile_picked_zcoref_soft_p_kernel(tc, x_words, x_scales, w1, ment, offs, ant,
                 out=z_codes[:].bitcast(FP8X4), scales=z_scales[:], in_=z_bf[i][:].rearrange("p n t -> p (n t)")
             )
             y_ps[i] = psum.tile([P, V], F32, name="y_ps%d" % i, tag="bank")
+            if i in TURNED:
+                for c in range(TILES):
+                    nc.tensor.matmul_mx(
+                        out=y_ps[i][:, c * P : (c + 1) * P],
+                        lhsT=ant_words[:, c * P : (c + 1) * P].bitcast(FP8X4),
+                        lhsT_scale=ant_scales[:, c * P : (c + 1) * P],
+                        rhs=z_codes[:].bitcast(FP8X4),
+                        rhs_scale=z_scales[:],
+                        start=True,
+                        stop=True,
+                    )
+                return
             nc.tensor.matmul_mx(
                 out=y_ps[i][:],
                 lhsT=z_codes[:].bitcast(FP8X4),
@@ -153,25 +180,38 @@ def tile_picked_zcoref_soft_p_kernel(tc, x_words, x_scales, w1, ment, offs, ant,
 
         def scores_direct(i):
             y_neg[i] = keep.tile([P, V], F32, name="y_neg%d" % i)
-            nc.vector.scalar_tensor_tensor(y_neg[i][:], y_ps[i][:], -1.0, ment_all, ALU.mult, ALU.subtract)
+            nc.vector.scalar_tensor_tensor(y_neg[i][:], y_ps[i][:], -1.0, ment_all, ALU.mult, ALU.add)
 
         def scores_staged(i):
             y_neg[i] = keep.tile([P, V], F32, name="y_neg%d" % i)
             staged = keep.tile([P, V], F32, name="staged%d" % i)
             nc.scalar.activation(staged[:], y_ps[i][:], ACT.Copy, scale=-1.0)
-            nc.gpsimd.tensor_tensor(y_neg[i][:], staged[:], ment_all, ALU.subtract)
+            nc.gpsimd.tensor_tensor(y_neg[i][:], staged[:], ment_all, ALU.add)
+
+        def scores_turned(i):
+            staged = keep.tile([P, V], F32, name="staged%d" % i)
+            nc.scalar.activation(staged[:], y_ps[i][:], ACT.Copy, scale=-1.0)
+            for c in range(TILES):
+                nc.tensor.matmul(
+                    y_neg[i][:, c * P : (c + 1) * P],
+                    staged[:, c * P : (c + 1) * P],
+                    ident[:],
+                    start=False,
+                    stop=c == TILES - 1,
+                    is_transpose=True,
+                )
 
         def row_max(i):
-            low[i] = keep.tile([P, 1], F32, name="low%d" % i, tag=HOLD.get(i, "low%d" % i))
+            low[i] = keep.tile([P, 1], F32, name="low%d" % i, tag=HOLD.get(i, "low%d" % i), align_bytes=64)
             nc.vector.tensor_reduce(low[i][:], y_neg[i][:], mybir.AxisListType.X, ALU.min)
 
         def exps(i):
             e[i] = keep.tile([P, V], F32, name="e%d" % i)
-            total[i] = keep.tile([P, 1], F32, name="total%d" % i, tag="total%d" % i)
+            total[i] = keep.tile([P, 1], F32, name="total%d" % i, tag="total%d" % i, align_bytes=64)
             nc.scalar.activation(e[i][:], y_neg[i][:], ACT.Exp, bias=low[i][:], scale=-1.0, accum_out=total[i][:])
 
         def invert(i):
-            invs[i] = keep.tile([P, 1], F32, name="inv%d" % i, tag="inv%d" % i)
+            invs[i] = keep.tile([P, 1], F32, name="inv%d" % i, tag="inv%d" % i, align_bytes=64)
             nc.vector.reciprocal(invs[i][:], total[i][:])
 
         def finish(i, engine):
@@ -189,21 +229,19 @@ def tile_picked_zcoref_soft_p_kernel(tc, x_words, x_scales, w1, ment, offs, ant,
         for i in range(TILES):
             second_product(i)
         scores_direct(0)
-        scores_staged(1)
-        scores_direct(2)
+        scores_turned(1)
+        scores_turned(2)
         row_max(0)
         exps(0)
         invert(0)
         finish(0, "gpsimd")
         scores_direct(3)
-        row_max(2)
-        exps(2)
-        for i in (1, 3):
+        for i in (1, 3, 2):
             row_max(i)
             exps(i)
-        invert(2)
         invert(1)
-        finish(2, "vector")
-        finish(1, "vector")
         invert(3)
+        finish(1, "vector")
         finish(3, "vector")
+        invert(2)
+        finish(2, "vector")

@@ -93,9 +93,9 @@ def tile_picked_zcoref_soft_p_kernel(tc, x_words, x_scales, w1, ment, offs, ant,
         nc.vector.tensor_copy(ant_scales[:], scale_win[:].indirect(ant_t[:]))
 
         w_bf = keep.tile([P, PACK, P, PACK], BF16, name="w_bf", align_bytes=64)
-        w_to = w_bf[:].rearrange("p t m j -> p m t j")
-        nc.scalar.copy(w_to[:, :CUT], w_raw[:].rearrange("p j (m t) -> p m t j", t=PACK))
-        nc.scalar.copy(w_to[:, CUT:], w_end[:].rearrange("p j (m t) -> p m t j", t=PACK))
+        w_to = w_bf[:].rearrange("p t m j -> p m j t")
+        nc.scalar.copy(w_to[:, :CUT], w_raw[:].rearrange("p j (m t) -> p m j t", t=PACK))
+        nc.scalar.copy(w_to[:, CUT:], w_end[:].rearrange("p j (m t) -> p m j t", t=PACK))
         w_codes = keep.tile([P, K], U32, name="w_codes", align_bytes=64)
         w_scales = keep.tile([P, K], U8, name="w_scales", align_bytes=64)
         for h in range(2):

@@ -36,9 +36,6 @@ def tile_picked_zcoref_soft_p_kernel(tc, x_words, x_scales, w1, ment, offs, ant,
         offs_t = keep.tile([P, S // GROUP], U16, name="offs_t")
         ant_t = keep.tile([P, V // GROUP], U16, name="ant_t")
         ment_win = keep.tile([P, T], F32, name="ment_win")
-        warm = keep.tile([P, 2], F32, name="warm")
-        nc.vector.memset(warm[:, 0:1], 0.0)
-        nc.scalar.activation(warm[:, 1:2], warm[:, 0:1], ACT.Exp)
         nc.vector.memset(ment_win[:ROW, :CLEAR], 0.0)
         nc.sync.dma_start(ant_t[:], ant)
         nc.sync.dma_start(ment_win[ROW:, :], ment[ROW:, :])

@@ -24,7 +24,7 @@ CUT = 80
 ROW = 127
 CLEAR = 1536
 TURNED = (1, 2)
-HOLD = {0: "z_bf3", 2: "total0"}
+HOLD = {0: "z_bf3", 3: "total0"}
 
 
 def tile_picked_zcoref_soft_p_kernel(tc, x_words, x_scales, w1, ment, offs, ant, out):
@@ -199,13 +199,18 @@ def tile_picked_zcoref_soft_p_kernel(tc, x_words, x_scales, w1, ment, offs, ant,
                 )
 
         def row_max(i):
-            low[i] = keep.tile([P, 1], F32, name="low%d" % i, tag=HOLD.get(i, "low%d" % i), align_bytes=64)
-            nc.vector.tensor_reduce(low[i][:], y_neg[i][:], mybir.AxisListType.X, ALU.min)
+            if i == 2:
+                low[2] = low[3][:, 1:2]
+                low[3] = low[3][:, 0:1]
+                nc.vector.tensor_reduce(low[i], y_neg[i][:], mybir.AxisListType.X, ALU.min)
+                return
+            low[i] = keep.tile([P, 2], F32, name="low%d" % i, tag=HOLD.get(i, "low%d" % i), align_bytes=64)
+            nc.vector.tensor_reduce(low[i][:, 0:1], y_neg[i][:], mybir.AxisListType.X, ALU.min)
 
         def exps(i):
             e[i] = keep.tile([P, V], F32, name="e%d" % i)
             total[i] = keep.tile([P, 1], F32, name="total%d" % i, tag="total%d" % i, align_bytes=64)
-            nc.scalar.activation(e[i][:], y_neg[i][:], ACT.Exp, bias=low[i][:], scale=-1.0, accum_out=total[i][:])
+            nc.scalar.activation(e[i][:], y_neg[i][:], ACT.Exp, bias=low[i][:, 0:1], scale=-1.0, accum_out=total[i][:])
 
         def invert(i):
             invs[i] = keep.tile([P, 1], F32, name="inv%d" % i, tag="inv%d" % i, align_bytes=64)

@@ -20,10 +20,11 @@ P = 128
 PACK = 4
 GROUP = 16
 TILES = S // P
-CUT = 80
+CUT = 64
 ROW = 127
 CLEAR = 1536
 TURNED = (1, 2)
+Z_BANK = ("y_neg2", "y_ps2", "y_ps3", "z_ps3")
 HOLD = {0: "z_bf3", 3: "total0"}
 
 
@@ -31,7 +32,7 @@ def tile_picked_zcoref_soft_p_kernel(tc, x_words, x_scales, w1, ment, offs, ant,
     nc = tc.nc
     with ExitStack() as ctx:
         keep = ctx.enter_context(tc.tile_pool(name="keep", bufs=1))
-        psum = ctx.enter_context(tc.psum_pool(name="psum", bufs=8))
+        psum = ctx.enter_context(tc.psum_pool(name="psum", bufs=1))
 
         offs_t = keep.tile([P, S // GROUP], U16, name="offs_t")
         ant_t = keep.tile([P, V // GROUP], U16, name="ant_t")
@@ -43,7 +44,6 @@ def tile_picked_zcoref_soft_p_kernel(tc, x_words, x_scales, w1, ment, offs, ant,
         w_raw = keep.tile([P, PACK, CUT * PACK], F32, name="w_raw")
         w_end = keep.tile([P, PACK, K - CUT * PACK], F32, name="w_end")
         nc.sync.dma_start(w_raw[:], w_rows[:, :, : CUT * PACK])
-        nc.sync.dma_start(offs_t[:], offs)
 
         scale_win = keep.tile([P, T], U8, name="scale_win", align_bytes=64)
         nc.gpsimd.memset(scale_win[:].bitcast(I32), 0)
@@ -52,26 +52,28 @@ def tile_picked_zcoref_soft_p_kernel(tc, x_words, x_scales, w1, ment, offs, ant,
             nc.sync.dma_start(scale_win[r:P:32, :].bitcast(I32), rows[r].bitcast(I32))
 
         nc.sync.dma_start(w_end[:], w_rows[:, :, CUT * PACK :])
+        nc.sync.dma_start(offs_t[:], offs)
         word_win = keep.tile([P, T], I32, name="word_win", align_bytes=64)
         nc.sync.dma_start(word_win[:], x_words[0].rearrange("p n t -> p (n t)").bitcast(I32))
 
+        nc.gpsimd.memset(ment_win[:ROW, CLEAR:], 0.0)
         ident = keep.tile([P, P], F32, name="ident")
         make_identity(nc, ident[:])
-        nc.gpsimd.memset(ment_win[:ROW, CLEAR:], 0.0)
 
         ment_row = keep.tile([P, V], F32, name="ment_row")
         nc.vector.tensor_copy(ment_row[:], ment_win[:].indirect(ant_t[:]))
-        turned = psum.tile([P, TILES, P], F32, name="turned", tag="bank")
+        turned = psum.tile([P, TILES, P], F32, name="turned", tag="turned")
         for c in range(TILES):
             nc.tensor.transpose(turned[:, c, :], ment_row[:, c * P : (c + 1) * P], ident[:])
         ment_col = keep.tile([P, TILES], F32, name="ment_col")
-        nc.scalar.activation(ment_col[:], turned[:, :, ROW], ACT.Copy, scale=-1.0)
-        spread = psum.tile([P, TILES, P], F32, name="spread", tag="bank")
+        nc.vector.tensor_scalar(ment_col[:], turned[:, :, ROW], -1.0, None, ALU.mult)
+        spread = psum.tile([P, TILES, P], F32, name="spread", tag="y_ps0")
         for c in range(TILES):
             nc.tensor.transpose(spread[:, c, :], ment_col[:, c : c + 1].to_broadcast([P, P]), ident[:])
         y_neg = {}
-        for i in TURNED:
-            y_neg[i] = psum.tile([P, V], F32, name="y_neg%d" % i, tag="bank")
+
+        def lay_ment(i):
+            y_neg[i] = psum.tile([P, V], F32, name="y_neg%d" % i, tag="y_neg%d" % i)
             for c in range(TILES):
                 nc.tensor.matmul(
                     y_neg[i][:, c * P : (c + 1) * P],
@@ -82,12 +84,14 @@ def tile_picked_zcoref_soft_p_kernel(tc, x_words, x_scales, w1, ment, offs, ant,
                     is_transpose=True,
                 )
 
+        lay_ment(1)
+
         span_scales = keep.tile([P, S], U8, name="span_scales", align_bytes=64)
         ant_scales = keep.tile([P, V], U8, name="ant_scales", align_bytes=64)
         span_words = [keep.tile([P, S // 2], U32, name="span_words%d" % h, align_bytes=64) for h in range(2)]
         ant_words = keep.tile([P, V], U32, name="ant_words", align_bytes=64)
-        nc.vector.tensor_copy(span_scales[:], scale_win[:].indirect(offs_t[:]))
         nc.vector.tensor_copy(ant_scales[:], scale_win[:].indirect(ant_t[:]))
+        nc.vector.tensor_copy(span_scales[:], scale_win[:].indirect(offs_t[:]))
 
         w_bf = keep.tile([P, PACK, P, PACK], BF16, name="w_bf", align_bytes=64)
         w_to = w_bf[:].rearrange("p t m j -> p m j t")
@@ -102,7 +106,7 @@ def tile_picked_zcoref_soft_p_kernel(tc, x_words, x_scales, w1, ment, offs, ant,
                 scales=w_scales[:, cols],
                 in_=w_bf[:, 2 * h : 2 * h + 2].rearrange("p t m j -> p (t m j)"),
             )
-        idle = psum.tile([P, K // 2], F32, name="idle", tag="bank")
+        idle = psum.tile([P, K // 2], F32, name="idle", tag="y_ps1")
         for c in range(4):
             nc.tensor.matmul_mx(
                 out=idle[:],
@@ -132,7 +136,7 @@ def tile_picked_zcoref_soft_p_kernel(tc, x_words, x_scales, w1, ment, offs, ant,
         invs = {}
 
         def first_product(i):
-            z_ps = psum.tile([P, PACK, P], F32, name="z_ps%d" % i, tag="bank")
+            z_ps = psum.tile([P, PACK, P], F32, name="z_ps%d" % i, tag=Z_BANK[i])
             for t in range(PACK):
                 nc.tensor.matmul_mx(
                     out=z_ps[:, t, :],
@@ -152,7 +156,7 @@ def tile_picked_zcoref_soft_p_kernel(tc, x_words, x_scales, w1, ment, offs, ant,
             nc.vector.quantize_mx(
                 out=z_codes[:].bitcast(FP8X4), scales=z_scales[:], in_=z_bf[i][:].rearrange("p n t -> p (n t)")
             )
-            y_ps[i] = psum.tile([P, V], F32, name="y_ps%d" % i, tag="bank")
+            y_ps[i] = psum.tile([P, V], F32, name="y_ps%d" % i, tag="y_ps%d" % i)
             if i in TURNED:
                 for c in range(TILES):
                     nc.tensor.matmul_mx(
@@ -228,6 +232,7 @@ def tile_picked_zcoref_soft_p_kernel(tc, x_words, x_scales, w1, ment, offs, ant,
 
         for i in range(TILES):
             first_product(i)
+        lay_ment(2)
         for i in range(TILES):
             second_product(i)
         scores_direct(0)

@@ -25,7 +25,7 @@ ROW = 127
 CLEAR = 1536
 TURNED = (1, 2)
 Z_BANK = ("y_neg2", "y_ps2", "y_ps3", "z_ps3")
-HOLD = {0: "z_bf3", 3: "total0"}
+HOLD = {0: "z_bf3", 3: "z_bf3"}
 
 
 def tile_picked_zcoref_soft_p_kernel(tc, x_words, x_scales, w1, ment, offs, ant, out):

@@ -180,7 +180,7 @@ def tile_picked_zcoref_soft_p_kernel(tc, x_words, x_scales, w1, ment, offs, ant,
             )
 
         def scores_direct(i):
-            y_neg[i] = keep.tile([P, V], F32, name="y_neg%d" % i)
+            y_neg[i] = keep.tile([P, V], F32, name="y_neg%d" % i, tag="scores%d" % i)
             nc.vector.scalar_tensor_tensor(y_neg[i][:], y_ps[i][:], -1.0, ment_all, ALU.mult, ALU.add)
 
         def scores_staged(i):
@@ -246,9 +246,22 @@ def tile_picked_zcoref_soft_p_kernel(tc, x_words, x_scales, w1, ment, offs, ant,
         for i in (1, 3, 2):
             row_max(i)
             exps(i)
+        half_v = V // 2
+
+        def finish_half(i, h, engine, tag):
+            cols = slice(h * half_v, (h + 1) * half_v)
+            res = keep.tile([P, half_v], F32, name=tag + "_res", tag=tag)
+            if engine == "vector":
+                nc.vector.tensor_scalar(res[:], e[i][:, cols], invs[i][:], None, ALU.mult)
+            else:
+                nc.scalar.activation(res[:], e[i][:, cols], ACT.Copy, scale=invs[i][:])
+            nc.sync.dma_start(out[i * P : (i + 1) * P, cols], res[:])
+
         invert(1)
+        finish_half(1, 0, "vector", "res1a")
         invert(3)
-        finish(1, "vector")
+        finish_half(1, 1, "vector", "scores3")
         finish(3, "vector")
         invert(2)
-        finish(2, "vector")
+        finish_half(2, 0, "vector", "res2a")
+        finish_half(2, 1, "scalar", "res2b")

@@ -25,7 +25,7 @@ ROW = 127
 CLEAR = 1536
 TURNED = (1, 2)
 Z_BANK = ("y_neg2", "y_ps2", "y_ps3", "z_ps3")
-HOLD = {0: "z_bf3", 3: "z_bf3"}
+HOLD = {0: "z_bf3", 2: "z_bf3", 3: "scores0"}
 
 
 def tile_picked_zcoref_soft_p_kernel(tc, x_words, x_scales, w1, ment, offs, ant, out):
@@ -180,7 +180,7 @@ def tile_picked_zcoref_soft_p_kernel(tc, x_words, x_scales, w1, ment, offs, ant,
             )
 
         def scores_direct(i):
-            y_neg[i] = keep.tile([P, V], F32, name="y_neg%d" % i, tag="scores%d" % i)
+            y_neg[i] = keep.tile([P, V], F32, name="y_neg%d" % i, tag="scores%d" % i, align_bytes=64)
             nc.vector.scalar_tensor_tensor(y_neg[i][:], y_ps[i][:], -1.0, ment_all, ALU.mult, ALU.add)
 
         def scores_staged(i):
@@ -203,11 +203,6 @@ def tile_picked_zcoref_soft_p_kernel(tc, x_words, x_scales, w1, ment, offs, ant,
                 )
 
         def row_max(i):
-            if i == 2:
-                low[2] = low[3][:, 1:2]
-                low[3] = low[3][:, 0:1]
-                nc.vector.tensor_reduce(low[i], y_neg[i][:], mybir.AxisListType.X, ALU.min)
-                return
             low[i] = keep.tile([P, 2], F32, name="low%d" % i, tag=HOLD.get(i, "low%d" % i), align_bytes=64)
             nc.vector.tensor_reduce(low[i][:, 0:1], y_neg[i][:], mybir.AxisListType.X, ALU.min)
 
@@ -243,14 +238,14 @@ def tile_picked_zcoref_soft_p_kernel(tc, x_words, x_scales, w1, ment, offs, ant,
         invert(0)
         finish(0, "gpsimd")
         scores_direct(3)
-        for i in (1, 3, 2):
+        for i in (1, 2, 3):
             row_max(i)
             exps(i)
         half_v = V // 2
 
         def finish_half(i, h, engine, tag):
             cols = slice(h * half_v, (h + 1) * half_v)
-            res = keep.tile([P, half_v], F32, name=tag + "_res", tag=tag)
+            res = keep.tile([P, half_v], F32, name=tag + "_res", tag=tag, align_bytes=64)
             if engine == "vector":
                 nc.vector.tensor_scalar(res[:], e[i][:, cols], invs[i][:], None, ALU.mult)
             else:
@@ -259,9 +254,9 @@ def tile_picked_zcoref_soft_p_kernel(tc, x_words, x_scales, w1, ment, offs, ant,
 
         invert(1)
         finish_half(1, 0, "vector", "res1a")
-        invert(3)
-        finish_half(1, 1, "vector", "scores3")
-        finish(3, "vector")
         invert(2)
-        finish_half(2, 0, "vector", "res2a")
-        finish_half(2, 1, "scalar", "res2b")
+        finish_half(1, 1, "vector", "z_bf3")
+        finish(2, "vector")
+        invert(3)
+        finish_half(3, 0, "vector", "res3a")
+        finish_half(3, 1, "scalar", "res3b")

@@ -148,7 +148,12 @@ def tile_picked_zcoref_soft_p_kernel(tc, x_words, x_scales, w1, ment, offs, ant,
                     stop=True,
                 )
             z_bf[i] = keep.tile([P, P, PACK], BF16, name="z_bf%d" % i, tag="z_bf%d" % i, align_bytes=64)
-            nc.scalar.copy(z_bf[i][:], z_ps[:].rearrange("p t n -> p n t"))
+            z_from = z_ps[:].rearrange("p t n -> p n t")
+            if i == 1:
+                nc.scalar.copy(z_bf[i][:, : P // 2], z_from[:, : P // 2])
+                nc.vector.tensor_copy(z_bf[i][:, P // 2 :], z_from[:, P // 2 :])
+            else:
+                nc.scalar.copy(z_bf[i][:], z_from)
 
         def second_product(i):
             z_codes = keep.tile([P, P], U32, name="z_codes%d" % i, align_bytes=64)

@@ -25,7 +25,7 @@ ROW = 127
 CLEAR = 1536
 TURNED = (1, 2)
 Z_BANK = ("y_neg2", "y_ps2", "y_ps3", "z_ps3")
-HOLD = {0: "z_bf3", 2: "z_bf3", 3: "scores0"}
+HOLD = {2: "low0", 3: "scores0"}
 
 
 def tile_picked_zcoref_soft_p_kernel(tc, x_words, x_scales, w1, ment, offs, ant, out):
@@ -161,6 +161,20 @@ def tile_picked_zcoref_soft_p_kernel(tc, x_words, x_scales, w1, ment, offs, ant,
             nc.vector.quantize_mx(
                 out=z_codes[:].bitcast(FP8X4), scales=z_scales[:], in_=z_bf[i][:].rearrange("p n t -> p (n t)")
             )
+            if i == 3:
+                y_ps[i] = [psum.tile([P, V // 2], F32, name="y_half%d" % h, tag=("y_ps3", "z_ps3")[h]) for h in range(2)]
+                for h in range(2):
+                    cols = slice(h * V // 2, (h + 1) * V // 2)
+                    nc.tensor.matmul_mx(
+                        out=y_ps[i][h][:],
+                        lhsT=z_codes[:].bitcast(FP8X4),
+                        lhsT_scale=z_scales[:],
+                        rhs=ant_words[:, cols].bitcast(FP8X4),
+                        rhs_scale=ant_scales[:, cols],
+                        start=True,
+                        stop=True,
+                    )
+                return
             y_ps[i] = psum.tile([P, V], F32, name="y_ps%d" % i, tag="y_ps%d" % i)
             if i in TURNED:
                 for c in range(TILES):
@@ -186,6 +200,13 @@ def tile_picked_zcoref_soft_p_kernel(tc, x_words, x_scales, w1, ment, offs, ant,
 
         def scores_direct(i):
             y_neg[i] = keep.tile([P, V], F32, name="y_neg%d" % i, tag="scores%d" % i, align_bytes=64)
+            if i == 3:
+                for h in range(2):
+                    cols = slice(h * V // 2, (h + 1) * V // 2)
+                    nc.vector.scalar_tensor_tensor(
+                        y_neg[i][:, cols], y_ps[i][h][:], -1.0, ment_all[:, cols], ALU.mult, ALU.add
+                    )
+                return
             nc.vector.scalar_tensor_tensor(y_neg[i][:], y_ps[i][:], -1.0, ment_all, ALU.mult, ALU.add)
 
         def scores_staged(i):
@@ -196,7 +217,10 @@ def tile_picked_zcoref_soft_p_kernel(tc, x_words, x_scales, w1, ment, offs, ant,
 
         def scores_turned(i):
             staged = keep.tile([P, V], F32, name="staged%d" % i)
-            nc.scalar.activation(staged[:], y_ps[i][:], ACT.Copy, scale=-1.0)
+            pieces = 2 if i == 1 else 1
+            for h in range(pieces):
+                cols = slice(h * V // pieces, (h + 1) * V // pieces)
+                nc.scalar.activation(staged[:, cols], y_ps[i][:, cols], ACT.Copy, scale=-1.0)
             for c in range(TILES):
                 nc.tensor.matmul(
                     y_neg[i][:, c * P : (c + 1) * P],
@@ -260,7 +284,7 @@ def tile_picked_zcoref_soft_p_kernel(tc, x_words, x_scales, w1, ment, offs, ant,
         invert(1)
         finish_half(1, 0, "vector", "res1a")
         invert(2)
-        finish_half(1, 1, "vector", "z_bf3")
+        finish_half(1, 1, "vector", "low0")
         finish(2, "vector")
         invert(3)
         finish_half(3, 0, "vector", "res3a")

@@ -21,6 +21,7 @@ PACK = 4
 GROUP = 16
 TILES = S // P
 CUT = 64
+SHARE = 108
 ROW = 127
 CLEAR = 1536
 TURNED = (1, 2)
@@ -96,7 +97,9 @@ def tile_picked_zcoref_soft_p_kernel(tc, x_words, x_scales, w1, ment, offs, ant,
         w_bf = keep.tile([P, PACK, P, PACK], BF16, name="w_bf", align_bytes=64)
         w_to = w_bf[:].rearrange("p t m j -> p m j t")
         nc.scalar.copy(w_to[:, :CUT], w_raw[:].rearrange("p j (m t) -> p m j t", t=PACK))
-        nc.scalar.copy(w_to[:, CUT:], w_end[:].rearrange("p j (m t) -> p m j t", t=PACK))
+        w_from = w_end[:].rearrange("p j (m t) -> p m j t", t=PACK)
+        nc.scalar.copy(w_to[:, CUT:SHARE], w_from[:, : SHARE - CUT])
+        nc.gpsimd.tensor_scalar(w_to[:, SHARE:], w_from[:, SHARE - CUT :], 1.0, 0.0, ALU.mult, ALU.add)
         w_codes = keep.tile([P, K], U32, name="w_codes", align_bytes=64)
         w_scales = keep.tile([P, K], U8, name="w_scales", align_bytes=64)
         for h in range(2):

@@ -61,13 +61,14 @@ def tile_picked_zcoref_soft_p_kernel(tc, x_words, x_scales, w1, ment, offs, ant,
         ident = keep.tile([P, P], F32, name="ident")
         make_identity(nc, ident[:])
 
-        ment_row = keep.tile([P, V], F32, name="ment_row")
-        nc.vector.tensor_copy(ment_row[:], ment_win[:].indirect(ant_t[:]))
+        w_area = keep.tile([P, K * PACK // 2 + V - P], F32, name="w_area", align_bytes=64)
+        ment_row = w_area[:, K * PACK // 2 - P :]
+        nc.vector.tensor_copy(ment_row, ment_win[:].indirect(ant_t[:]))
         turned = psum.tile([P, TILES, P], F32, name="turned", tag="turned")
-        for c in range(TILES):
+        for c in reversed(range(TILES)):
             nc.tensor.transpose(turned[:, c, :], ment_row[:, c * P : (c + 1) * P], ident[:])
         ment_col = keep.tile([P, TILES], F32, name="ment_col")
-        nc.vector.tensor_scalar(ment_col[:], turned[:, :, ROW], -1.0, None, ALU.mult)
+        nc.scalar.activation(ment_col[:], turned[:, :, ROW], ACT.Copy, scale=-1.0)
         spread = psum.tile([P, TILES, P], F32, name="spread", tag="y_ps0")
         for c in range(TILES):
             nc.tensor.transpose(spread[:, c, :], ment_col[:, c : c + 1].to_broadcast([P, P]), ident[:])
@@ -94,12 +95,19 @@ def tile_picked_zcoref_soft_p_kernel(tc, x_words, x_scales, w1, ment, offs, ant,
         nc.vector.tensor_copy(ant_scales[:], scale_win[:].indirect(ant_t[:]))
         nc.vector.tensor_copy(span_scales[:], scale_win[:].indirect(offs_t[:]))
 
-        w_bf = keep.tile([P, PACK, P, PACK], BF16, name="w_bf", align_bytes=64)
-        w_to = w_bf[:].rearrange("p t m j -> p m j t")
+        w_bf = w_area[:, : K * PACK // 2].bitcast(BF16).rearrange("p (t m j) -> p t m j", t=PACK, j=PACK)
+        w_to = w_bf.rearrange("p t m j -> p m j t")
         nc.scalar.copy(w_to[:, :CUT], w_raw[:].rearrange("p j (m t) -> p m j t", t=PACK))
         w_from = w_end[:].rearrange("p j (m t) -> p m j t", t=PACK)
         nc.scalar.copy(w_to[:, CUT:SHARE], w_from[:, : SHARE - CUT])
-        nc.gpsimd.tensor_scalar(w_to[:, SHARE:], w_from[:, SHARE - CUT :], 1.0, 0.0, ALU.mult, ALU.add)
+        nc.gpsimd.tensor_scalar(
+            w_bf[:, :, SHARE:, :].rearrange("p t m j -> p m t j"),
+            w_end[:].rearrange("p j (m t) -> p m t j", t=PACK)[:, SHARE - CUT :],
+            1.0,
+            0.0,
+            ALU.mult,
+            ALU.add,
+        )
         w_codes = keep.tile([P, K], U32, name="w_codes", align_bytes=64)
         w_scales = keep.tile([P, K], U8, name="w_scales", align_bytes=64)
         for h in range(2):

@@ -21,12 +21,14 @@ PACK = 4
 GROUP = 16
 TILES = S // P
 CUT = 64
+FIRST = 48
 SHARE = 108
 ROW = 127
 CLEAR = 1536
 TURNED = (1, 2)
-Z_BANK = ("y_neg2", "y_ps2", "y_ps3", "z_ps3")
-HOLD = {2: "low0", 3: "scores0"}
+Z_BANK = ("turned", "y_ps2", "y_ps3", "z_ps3")
+HOLD = {1: "low0", 3: "scores0"}
+OWN = 32
 
 
 def tile_picked_zcoref_soft_p_kernel(tc, x_words, x_scales, w1, ment, offs, ant, out):
@@ -61,14 +63,23 @@ def tile_picked_zcoref_soft_p_kernel(tc, x_words, x_scales, w1, ment, offs, ant,
         ident = keep.tile([P, P], F32, name="ident")
         make_identity(nc, ident[:])
 
-        w_area = keep.tile([P, K * PACK // 2 + V - P], F32, name="w_area", align_bytes=64)
-        ment_row = w_area[:, K * PACK // 2 - P :]
-        nc.vector.tensor_copy(ment_row, ment_win[:].indirect(ant_t[:]))
+        row_at = ((PACK - 1) * P + FIRST) * PACK // 2
+        w_area = keep.tile([P, row_at + V], F32, name="w_area", align_bytes=64)
+        ment_row = w_area[:, row_at:]
+        for h in (1, 0):
+            nc.vector.tensor_copy(
+                ment_row[:, h * V // 2 : (h + 1) * V // 2],
+                ment_win[:].indirect(ant_t[:, h * V // GROUP // 2 : (h + 1) * V // GROUP // 2]),
+            )
         turned = psum.tile([P, TILES, P], F32, name="turned", tag="turned")
         for c in reversed(range(TILES)):
             nc.tensor.transpose(turned[:, c, :], ment_row[:, c * P : (c + 1) * P], ident[:])
-        ment_col = keep.tile([P, TILES], F32, name="ment_col")
-        nc.scalar.activation(ment_col[:], turned[:, :, ROW], ACT.Copy, scale=-1.0)
+        w_bf = w_area[:, : K * PACK // 2].bitcast(BF16).rearrange("p (t m j) -> p t m j", t=PACK, j=PACK)
+        w_to = w_bf.rearrange("p t m j -> p m j t")
+        w_head = w_raw[:].rearrange("p j (m t) -> p m j t", t=PACK)
+        nc.scalar.copy(w_to[:, :FIRST], w_head[:, :FIRST])
+        ment_col = w_raw[:, 0, :TILES]
+        nc.scalar.activation(ment_col, turned[:, :, ROW], ACT.Copy, scale=-1.0)
         spread = psum.tile([P, TILES, P], F32, name="spread", tag="y_ps0")
         for c in range(TILES):
             nc.tensor.transpose(spread[:, c, :], ment_col[:, c : c + 1].to_broadcast([P, P]), ident[:])
@@ -87,6 +98,7 @@ def tile_picked_zcoref_soft_p_kernel(tc, x_words, x_scales, w1, ment, offs, ant,
                 )
 
         lay_ment(1)
+        lay_ment(2)
 
         span_scales = keep.tile([P, S], U8, name="span_scales", align_bytes=64)
         ant_scales = keep.tile([P, V], U8, name="ant_scales", align_bytes=64)
@@ -95,9 +107,7 @@ def tile_picked_zcoref_soft_p_kernel(tc, x_words, x_scales, w1, ment, offs, ant,
         nc.vector.tensor_copy(ant_scales[:], scale_win[:].indirect(ant_t[:]))
         nc.vector.tensor_copy(span_scales[:], scale_win[:].indirect(offs_t[:]))
 
-        w_bf = w_area[:, : K * PACK // 2].bitcast(BF16).rearrange("p (t m j) -> p t m j", t=PACK, j=PACK)
-        w_to = w_bf.rearrange("p t m j -> p m j t")
-        nc.scalar.copy(w_to[:, :CUT], w_raw[:].rearrange("p j (m t) -> p m j t", t=PACK))
+        nc.scalar.copy(w_to[:, FIRST:CUT], w_head[:, FIRST:])
         w_from = w_end[:].rearrange("p j (m t) -> p m j t", t=PACK)
         nc.scalar.copy(w_to[:, CUT:SHARE], w_from[:, : SHARE - CUT])
         nc.gpsimd.tensor_scalar(
@@ -140,6 +150,7 @@ def tile_picked_zcoref_soft_p_kernel(tc, x_words, x_scales, w1, ment, offs, ant,
         nc.vector.tensor_copy(ant_words[:], word_win[:].bitcast(U32).indirect(ant_t[:]))
 
         z_bf = {}
+        rest = {}
         y_ps = {}
         low = {}
         e = {}
@@ -161,8 +172,8 @@ def tile_picked_zcoref_soft_p_kernel(tc, x_words, x_scales, w1, ment, offs, ant,
             z_bf[i] = keep.tile([P, P, PACK], BF16, name="z_bf%d" % i, tag="z_bf%d" % i, align_bytes=64)
             z_from = z_ps[:].rearrange("p t n -> p n t")
             if i == 1:
-                nc.scalar.copy(z_bf[i][:, : P // 2], z_from[:, : P // 2])
-                nc.vector.tensor_copy(z_bf[i][:, P // 2 :], z_from[:, P // 2 :])
+                nc.scalar.copy(z_bf[i][:, :OWN], z_from[:, :OWN])
+                rest[i] = z_from[:, OWN:]
             else:
                 nc.scalar.copy(z_bf[i][:], z_from)
 
@@ -228,7 +239,7 @@ def tile_picked_zcoref_soft_p_kernel(tc, x_words, x_scales, w1, ment, offs, ant,
 
         def scores_turned(i):
             staged = keep.tile([P, V], F32, name="staged%d" % i)
-            pieces = 2 if i == 1 else 1
+            pieces = 2 if i == 2 else 1
             for h in range(pieces):
                 cols = slice(h * V // pieces, (h + 1) * V // pieces)
                 nc.scalar.activation(staged[:, cols], y_ps[i][:, cols], ACT.Copy, scale=-1.0)
@@ -267,18 +278,19 @@ def tile_picked_zcoref_soft_p_kernel(tc, x_words, x_scales, w1, ment, offs, ant,
 
         for i in range(TILES):
             first_product(i)
-        lay_ment(2)
-        for i in range(TILES):
+        second_product(0)
+        nc.vector.tensor_copy(z_bf[1][:, OWN:], rest[1])
+        for i in (2, 1, 3):
             second_product(i)
         scores_direct(0)
-        scores_turned(1)
         scores_turned(2)
+        scores_turned(1)
         row_max(0)
         exps(0)
         invert(0)
         finish(0, "gpsimd")
         scores_direct(3)
-        for i in (1, 2, 3):
+        for i in (2, 1, 3):
             row_max(i)
             exps(i)
         half_v = V // 2
@@ -292,11 +304,11 @@ def tile_picked_zcoref_soft_p_kernel(tc, x_words, x_scales, w1, ment, offs, ant,
                 nc.scalar.activation(res[:], e[i][:, cols], ACT.Copy, scale=invs[i][:])
             nc.sync.dma_start(out[i * P : (i + 1) * P, cols], res[:])
 
-        invert(1)
-        finish_half(1, 0, "vector", "res1a")
         invert(2)
-        finish_half(1, 1, "vector", "low0")
-        finish(2, "vector")
+        finish_half(2, 0, "vector", "res2a")
+        invert(1)
+        finish_half(2, 1, "vector", "low0")
+        finish(1, "vector")
         invert(3)
         finish_half(3, 0, "vector", "res3a")
         finish_half(3, 1, "scalar", "res3b")

@@ -127,18 +127,6 @@ def tile_picked_zcoref_soft_p_kernel(tc, x_words, x_scales, w1, ment, offs, ant,
                 scales=w_scales[:, cols],
                 in_=w_bf[:, 2 * h : 2 * h + 2].rearrange("p t m j -> p (t m j)"),
             )
-        idle = psum.tile([P, K // 2], F32, name="idle", tag="y_ps1")
-        for c in range(4):
-            nc.tensor.matmul_mx(
-                out=idle[:],
-                lhsT=w_codes[:, :P].bitcast(FP8X4),
-                lhsT_scale=w_scales[:, :P],
-                rhs=w_codes[:, : K // 2].bitcast(FP8X4),
-                rhs_scale=w_scales[:, : K // 2],
-                start=True,
-                stop=True,
-            )
-
         ment_all = w_end[:].rearrange("p j c -> p (j c)")[:, :V]
         nc.scalar.copy(ment_all, spread[:].rearrange("p c n -> p (c n)"))
 

@@ -29,6 +29,7 @@ TURNED = (1, 2)
 Z_BANK = ("turned", "y_ps2", "y_ps3", "z_ps3")
 HOLD = {1: "low0", 3: "scores0"}
 OWN = 32
+SPAN_CUTS = ((0, P), (P, 3 * P), (3 * P, S))
 
 
 def tile_picked_zcoref_soft_p_kernel(tc, x_words, x_scales, w1, ment, offs, ant, out):
@@ -102,8 +103,7 @@ def tile_picked_zcoref_soft_p_kernel(tc, x_words, x_scales, w1, ment, offs, ant,
 
         span_scales = keep.tile([P, S], U8, name="span_scales", align_bytes=64)
         ant_scales = keep.tile([P, V], U8, name="ant_scales", align_bytes=64)
-        span_words = [keep.tile([P, S // 2], U32, name="span_words%d" % h, align_bytes=64) for h in range(2)]
-        ant_words = keep.tile([P, V], U32, name="ant_words", align_bytes=64)
+        span_words = keep.tile([P, S], U32, name="span_words", align_bytes=64)
         nc.vector.tensor_copy(ant_scales[:], scale_win[:].indirect(ant_t[:]))
         nc.vector.tensor_copy(span_scales[:], scale_win[:].indirect(offs_t[:]))
 
@@ -130,11 +130,11 @@ def tile_picked_zcoref_soft_p_kernel(tc, x_words, x_scales, w1, ment, offs, ant,
         ment_all = w_end[:].rearrange("p j c -> p (j c)")[:, :V]
         nc.scalar.copy(ment_all, spread[:].rearrange("p c n -> p (c n)"))
 
-        half = S // GROUP // 2
-        for h in range(2):
+        for a, b in SPAN_CUTS:
             nc.vector.tensor_copy(
-                span_words[h][:], word_win[:].bitcast(U32).indirect(offs_t[:, h * half : (h + 1) * half])
+                span_words[:, a:b], word_win[:].bitcast(U32).indirect(offs_t[:, a // GROUP : b // GROUP])
             )
+        ant_words = keep.tile([P, V], U32, name="ant_words", align_bytes=64)
         nc.vector.tensor_copy(ant_words[:], word_win[:].bitcast(U32).indirect(ant_t[:]))
 
         z_bf = {}
@@ -152,7 +152,7 @@ def tile_picked_zcoref_soft_p_kernel(tc, x_words, x_scales, w1, ment, offs, ant,
                     out=z_ps[:, t, :],
                     lhsT=w_codes[:, t * P : (t + 1) * P].bitcast(FP8X4),
                     lhsT_scale=w_scales[:, t * P : (t + 1) * P],
-                    rhs=span_words[i // 2][:, (i % 2) * P : (i % 2 + 1) * P].bitcast(FP8X4),
+                    rhs=span_words[:, i * P : (i + 1) * P].bitcast(FP8X4),
                     rhs_scale=span_scales[:, i * P : (i + 1) * P],
                     start=True,
                     stop=True,

@@ -219,18 +219,9 @@ def tile_picked_zcoref_soft_p_kernel(tc, x_words, x_scales, w1, ment, offs, ant,
                 return
             nc.vector.scalar_tensor_tensor(y_neg[i][:], y_ps[i][:], -1.0, ment_all, ALU.mult, ALU.add)
 
-        def scores_staged(i):
-            y_neg[i] = keep.tile([P, V], F32, name="y_neg%d" % i)
-            staged = keep.tile([P, V], F32, name="staged%d" % i)
-            nc.scalar.activation(staged[:], y_ps[i][:], ACT.Copy, scale=-1.0)
-            nc.gpsimd.tensor_tensor(y_neg[i][:], staged[:], ment_all, ALU.add)
-
         def scores_turned(i):
             staged = keep.tile([P, V], F32, name="staged%d" % i)
-            pieces = 2 if i == 2 else 1
-            for h in range(pieces):
-                cols = slice(h * V // pieces, (h + 1) * V // pieces)
-                nc.scalar.activation(staged[:, cols], y_ps[i][:, cols], ACT.Copy, scale=-1.0)
+            nc.scalar.activation(staged[:], y_ps[i][:], ACT.Copy, scale=-1.0)
             for c in range(TILES):
                 nc.tensor.matmul(
                     y_neg[i][:, c * P : (c + 1) * P],

from contextlib import ExitStack

import concourse.mybir as mybir
from concourse.masks import make_identity

K, T, S, V = 512, 2048, 512, 512
FLOPS = 2 * K * K * S + 2 * K * S * V

F32 = mybir.dt.float32
BF16 = mybir.dt.bfloat16
I32 = mybir.dt.int32
U32 = mybir.dt.uint32
U16 = mybir.dt.uint16
U8 = mybir.dt.uint8
FP8X4 = mybir.dt.float8_e4m3fn_x4
ALU = mybir.AluOpType
ACT = mybir.ActivationFunctionType

P = 128
PACK = 4
GROUP = 16
TILES = S // P
CUT = 64
FIRST = 48
SHARE = 108
ROW = 127
CLEAR = 1536
TURNED = (1, 2)
Z_BANK = ("turned", "y_ps2", "y_ps3", "z_ps3")
HOLD = {1: "low0", 3: "scores0"}
OWN = 32
SPAN_CUTS = ((0, P), (P, 3 * P), (3 * P, S))


def tile_picked_zcoref_soft_p_kernel(tc, x_words, x_scales, w1, ment, offs, ant, out):
    nc = tc.nc
    with ExitStack() as ctx:
        keep = ctx.enter_context(tc.tile_pool(name="keep", bufs=1))
        psum = ctx.enter_context(tc.psum_pool(name="psum", bufs=1))

        offs_t = keep.tile([P, S // GROUP], U16, name="offs_t")
        ant_t = keep.tile([P, V // GROUP], U16, name="ant_t")
        ment_win = keep.tile([P, T], F32, name="ment_win")
        nc.vector.memset(ment_win[:ROW, :CLEAR], 0.0)
        nc.sync.dma_start(ant_t[:], ant)
        nc.sync.dma_start(ment_win[ROW:, :], ment[ROW:, :])
        w_rows = w1.rearrange("(p j) c -> p j c", j=PACK)
        w_raw = keep.tile([P, PACK, CUT * PACK], F32, name="w_raw")
        w_end = keep.tile([P, PACK, K - CUT * PACK], F32, name="w_end")
        nc.sync.dma_start(w_raw[:], w_rows[:, :, : CUT * PACK])

        scale_win = keep.tile([P, T], U8, name="scale_win", align_bytes=64)
        nc.gpsimd.memset(scale_win[:].bitcast(I32), 0)
        rows = x_scales[0].rearrange("(q r) c -> r q c", r=4)
        for r in range(4):
            nc.sync.dma_start(scale_win[r:P:32, :].bitcast(I32), rows[r].bitcast(I32))

        nc.sync.dma_start(w_end[:], w_rows[:, :, CUT * PACK :])
        nc.sync.dma_start(offs_t[:], offs)
        word_win = keep.tile([P, T], I32, name="word_win", align_bytes=64)
        nc.sync.dma_start(word_win[:], x_words[0].rearrange("p n t -> p (n t)").bitcast(I32))

        nc.gpsimd.memset(ment_win[:ROW, CLEAR:], 0.0)
        ident = keep.tile([P, P], F32, name="ident")
        make_identity(nc, ident[:])

        row_at = ((PACK - 1) * P + FIRST) * PACK // 2
        w_area = keep.tile([P, row_at + V], F32, name="w_area", align_bytes=64)
        ment_row = w_area[:, row_at:]
        for h in (1, 0):
            nc.vector.tensor_copy(
                ment_row[:, h * V // 2 : (h + 1) * V // 2],
                ment_win[:].indirect(ant_t[:, h * V // GROUP // 2 : (h + 1) * V // GROUP // 2]),
            )
        turned = psum.tile([P, TILES, P], F32, name="turned", tag="turned")
        for c in reversed(range(TILES)):
            nc.tensor.transpose(turned[:, c, :], ment_row[:, c * P : (c + 1) * P], ident[:])
        w_bf = w_area[:, : K * PACK // 2].bitcast(BF16).rearrange("p (t m j) -> p t m j", t=PACK, j=PACK)
        w_to = w_bf.rearrange("p t m j -> p m j t")
        w_head = w_raw[:].rearrange("p j (m t) -> p m j t", t=PACK)
        nc.scalar.copy(w_to[:, :FIRST], w_head[:, :FIRST])
        ment_col = w_raw[:, 0, :TILES]
        nc.scalar.activation(ment_col, turned[:, :, ROW], ACT.Copy, scale=-1.0)
        spread = psum.tile([P, TILES, P], F32, name="spread", tag="y_ps0")
        for c in range(TILES):
            nc.tensor.transpose(spread[:, c, :], ment_col[:, c : c + 1].to_broadcast([P, P]), ident[:])
        y_neg = {}

        def lay_ment(i):
            y_neg[i] = psum.tile([P, V], F32, name="y_neg%d" % i, tag="y_neg%d" % i)
            for c in range(TILES):
                nc.tensor.matmul(
                    y_neg[i][:, c * P : (c + 1) * P],
                    ment_col[:, c : c + 1].to_broadcast([P, P]),
                    ident[:],
                    start=c == 0,
                    stop=False,
                    is_transpose=True,
                )

        lay_ment(1)
        lay_ment(2)

        span_scales = keep.tile([P, S], U8, name="span_scales", align_bytes=64)
        ant_scales = keep.tile([P, V], U8, name="ant_scales", align_bytes=64)
        span_words = keep.tile([P, S], U32, name="span_words", align_bytes=64)
        nc.vector.tensor_copy(ant_scales[:], scale_win[:].indirect(ant_t[:]))
        nc.vector.tensor_copy(span_scales[:], scale_win[:].indirect(offs_t[:]))

        nc.scalar.copy(w_to[:, FIRST:CUT], w_head[:, FIRST:])
        w_from = w_end[:].rearrange("p j (m t) -> p m j t", t=PACK)
        nc.scalar.copy(w_to[:, CUT:SHARE], w_from[:, : SHARE - CUT])
        nc.gpsimd.tensor_scalar(
            w_bf[:, :, SHARE:, :].rearrange("p t m j -> p m t j"),
            w_end[:].rearrange("p j (m t) -> p m t j", t=PACK)[:, SHARE - CUT :],
            1.0,
            0.0,
            ALU.mult,
            ALU.add,
        )
        w_codes = keep.tile([P, K], U32, name="w_codes", align_bytes=64)
        w_scales = keep.tile([P, K], U8, name="w_scales", align_bytes=64)
        for h in range(2):
            cols = slice(h * K // 2, (h + 1) * K // 2)
            nc.vector.quantize_mx(
                out=w_codes[:, cols].bitcast(FP8X4),
                scales=w_scales[:, cols],
                in_=w_bf[:, 2 * h : 2 * h + 2].rearrange("p t m j -> p (t m j)"),
            )
        ment_all = w_end[:].rearrange("p j c -> p (j c)")[:, :V]
        nc.scalar.copy(ment_all, spread[:].rearrange("p c n -> p (c n)"))

        for a, b in SPAN_CUTS:
            nc.vector.tensor_copy(
                span_words[:, a:b], word_win[:].bitcast(U32).indirect(offs_t[:, a // GROUP : b // GROUP])
            )
        ant_words = keep.tile([P, V], U32, name="ant_words", align_bytes=64)
        nc.vector.tensor_copy(ant_words[:], word_win[:].bitcast(U32).indirect(ant_t[:]))

        z_bf = {}
        rest = {}
        y_ps = {}
        low = {}
        e = {}
        total = {}
        invs = {}

        def first_product(i):
            z_ps = psum.tile([P, PACK, P], F32, name="z_ps%d" % i, tag=Z_BANK[i])
            for t in range(PACK):
                nc.tensor.matmul_mx(
                    out=z_ps[:, t, :],
                    lhsT=w_codes[:, t * P : (t + 1) * P].bitcast(FP8X4),
                    lhsT_scale=w_scales[:, t * P : (t + 1) * P],
                    rhs=span_words[:, i * P : (i + 1) * P].bitcast(FP8X4),
                    rhs_scale=span_scales[:, i * P : (i + 1) * P],
                    start=True,
                    stop=True,
                )
            z_bf[i] = keep.tile([P, P, PACK], BF16, name="z_bf%d" % i, tag="z_bf%d" % i, align_bytes=64)
            z_from = z_ps[:].rearrange("p t n -> p n t")
            if i == 1:
                nc.scalar.copy(z_bf[i][:, :OWN], z_from[:, :OWN])
                rest[i] = z_from[:, OWN:]
            else:
                nc.scalar.copy(z_bf[i][:], z_from)

        def second_product(i):
            z_codes = keep.tile([P, P], U32, name="z_codes%d" % i, align_bytes=64)
            z_scales = keep.tile([P, P], U8, name="z_scales%d" % i, align_bytes=64)
            nc.vector.quantize_mx(
                out=z_codes[:].bitcast(FP8X4), scales=z_scales[:], in_=z_bf[i][:].rearrange("p n t -> p (n t)")
            )
            if i == 3:
                y_ps[i] = [psum.tile([P, V // 2], F32, name="y_half%d" % h, tag=("y_ps3", "z_ps3")[h]) for h in range(2)]
                for h in range(2):
                    cols = slice(h * V // 2, (h + 1) * V // 2)
                    nc.tensor.matmul_mx(
                        out=y_ps[i][h][:],
                        lhsT=z_codes[:].bitcast(FP8X4),
                        lhsT_scale=z_scales[:],
                        rhs=ant_words[:, cols].bitcast(FP8X4),
                        rhs_scale=ant_scales[:, cols],
                        start=True,
                        stop=True,
                    )
                return
            y_ps[i] = psum.tile([P, V], F32, name="y_ps%d" % i, tag="y_ps%d" % i)
            if i in TURNED:
                for c in range(TILES):
                    nc.tensor.matmul_mx(
                        out=y_ps[i][:, c * P : (c + 1) * P],
                        lhsT=ant_words[:, c * P : (c + 1) * P].bitcast(FP8X4),
                        lhsT_scale=ant_scales[:, c * P : (c + 1) * P],
                        rhs=z_codes[:].bitcast(FP8X4),
                        rhs_scale=z_scales[:],
                        start=True,
                        stop=True,
                    )
                return
            nc.tensor.matmul_mx(
                out=y_ps[i][:],
                lhsT=z_codes[:].bitcast(FP8X4),
                lhsT_scale=z_scales[:],
                rhs=ant_words[:].bitcast(FP8X4),
                rhs_scale=ant_scales[:],
                start=True,
                stop=True,
            )

        def scores_direct(i):
            y_neg[i] = keep.tile([P, V], F32, name="y_neg%d" % i, tag="scores%d" % i, align_bytes=64)
            if i == 3:
                for h in range(2):
                    cols = slice(h * V // 2, (h + 1) * V // 2)
                    nc.vector.scalar_tensor_tensor(
                        y_neg[i][:, cols], y_ps[i][h][:], -1.0, ment_all[:, cols], ALU.mult, ALU.add
                    )
                return
            nc.vector.scalar_tensor_tensor(y_neg[i][:], y_ps[i][:], -1.0, ment_all, ALU.mult, ALU.add)

        def scores_turned(i):
            staged = keep.tile([P, V], F32, name="staged%d" % i)
            nc.scalar.activation(staged[:], y_ps[i][:], ACT.Copy, scale=-1.0)
            for c in range(TILES):
                nc.tensor.matmul(
                    y_neg[i][:, c * P : (c + 1) * P],
                    staged[:, c * P : (c + 1) * P],
                    ident[:],
                    start=False,
                    stop=c == TILES - 1,
                    is_transpose=True,
                )

        def row_max(i):
            low[i] = keep.tile([P, 2], F32, name="low%d" % i, tag=HOLD.get(i, "low%d" % i), align_bytes=64)
            nc.vector.tensor_reduce(low[i][:, 0:1], y_neg[i][:], mybir.AxisListType.X, ALU.min)

        def exps(i):
            e[i] = keep.tile([P, V], F32, name="e%d" % i)
            total[i] = keep.tile([P, 1], F32, name="total%d" % i, tag="total%d" % i, align_bytes=64)
            nc.scalar.activation(e[i][:], y_neg[i][:], ACT.Exp, bias=low[i][:, 0:1], scale=-1.0, accum_out=total[i][:])

        def invert(i):
            invs[i] = keep.tile([P, 1], F32, name="inv%d" % i, tag="inv%d" % i, align_bytes=64)
            nc.vector.reciprocal(invs[i][:], total[i][:])

        def finish(i, engine):
            res = keep.tile([P, V], F32, name="res%d" % i)
            if engine == "vector":
                nc.vector.tensor_scalar(res[:], e[i][:], invs[i][:], None, ALU.mult)
            elif engine == "scalar":
                nc.scalar.activation(res[:], e[i][:], ACT.Copy, scale=invs[i][:])
            else:
                nc.gpsimd.tensor_scalar(res[:], e[i][:], invs[i][:], 0.0, ALU.mult, ALU.add)
            nc.sync.dma_start(out[i * P : (i + 1) * P, :], res[:])

        for i in range(TILES):
            first_product(i)
        second_product(0)
        nc.vector.tensor_copy(z_bf[1][:, OWN:], rest[1])
        for i in (2, 1, 3):
            second_product(i)
        scores_direct(0)
        scores_turned(2)
        scores_turned(1)
        row_max(0)
        exps(0)
        invert(0)
        finish(0, "gpsimd")
        scores_direct(3)
        for i in (2, 1, 3):
            row_max(i)
            exps(i)
        half_v = V // 2

        def finish_half(i, h, engine, tag):
            cols = slice(h * half_v, (h + 1) * half_v)
            res = keep.tile([P, half_v], F32, name=tag + "_res", tag=tag, align_bytes=64)
            if engine == "vector":
                nc.vector.tensor_scalar(res[:], e[i][:, cols], invs[i][:], None, ALU.mult)
            else:
                nc.scalar.activation(res[:], e[i][:, cols], ACT.Copy, scale=invs[i][:])
            nc.sync.dma_start(out[i * P : (i + 1) * P, cols], res[:])

        invert(2)
        finish_half(2, 0, "vector", "res2a")
        invert(1)
        finish_half(2, 1, "vector", "low0")
        finish(1, "vector")
        invert(3)
        finish_half(3, 0, "vector", "res3a")
        finish_half(3, 1, "scalar", "res3b")
